import numpy as np
import ml_dtypes


def mxq(x, axis, fmt="e4m3"):
    dtype, down = {"e4m3": (ml_dtypes.float8_e4m3fn, 7), "e5m2": (ml_dtypes.float8_e5m2, 14)}[fmt]
    v = np.moveaxis(np.asarray(x, np.float32).astype(ml_dtypes.bfloat16).astype(np.float64), axis, -1)
    blocks = v.reshape(v.shape[:-1] + (-1, 32))
    amax = np.abs(blocks).max(-1, keepdims=True)
    byte = np.maximum(np.where(amax > 0, np.frexp(amax)[1] - 1 + 127, 0) - down, 1)
    scale = np.exp2(byte - 127.0)
    codes = (blocks / scale).astype(np.float32).astype(dtype).astype(np.float64)
    return np.moveaxis((codes * scale).reshape(v.shape), -1, axis)


WIDE = False


def mx_kscale(k):
    if not WIDE:
        return np.ones(k)
    levels = np.array([10, -10, 5, -5, 0])
    if k % 512:
        return np.exp2(np.random.permutation(np.resize(levels, k // 32))).repeat(32)
    a = np.empty((k // 512, 16))
    for p in range(k // 512):
        a[p, :8] = np.random.permutation(np.resize(levels, 8))
        for g in range(8):
            far = levels[np.abs(levels - a[p, g]) >= 10]
            a[p, g + 8] = far[np.random.randint(len(far))]
    return np.exp2(a.ravel()).repeat(32)


def f64(x):
    return np.asarray(x).astype(np.float64)


def striped(idx):
    return np.tile(idx.reshape(-1, 16).T, (8, 1)).astype(np.uint16)


def unstriped(offs):
    return offs[:16].T.reshape(-1).astype(np.int64)


def striped8(idx):
    return np.concatenate([x.reshape(-1, 16).T for x in idx]).astype(np.uint16)


def runs(offs, k):
    lists = np.stack([offs[16 * r : 16 * r + 16].T.reshape(-1) for r in range(8)]).astype(np.int64)
    return lists[np.arange(k) % 512 // 64]


def pack_weight(w):
    k, n = w.shape
    w = f64(np.asarray(w, np.float32).astype(ml_dtypes.bfloat16)).reshape(k // 32, 32, n)
    amax = np.abs(w).max(1)
    byte = np.clip(np.where(amax > 0, np.frexp(amax)[1] - 1 + 127 - 7, 1), 1, 254)
    scaled = (w * np.exp2(127.0 - byte)[:, None, :]).reshape(k, n).astype(np.float32)
    words = np.ascontiguousarray(scaled.reshape(k // 512, 128, 4, n).transpose(0, 1, 3, 2)).astype(ml_dtypes.float8_e4m3fn).view(np.uint8)
    return words, np.ascontiguousarray(byte.astype(np.uint8).reshape(k // 512, 16, n))


def unpack_weight(words, scales):
    g, p, n, _ = words.shape
    vals = np.ascontiguousarray(words).view(ml_dtypes.float8_e4m3fn).astype(np.float64) * np.repeat(np.exp2(scales.astype(np.float64) - 127.0), 8, axis=1)[..., None]
    return vals.transpose(0, 1, 3, 2).reshape(g * 512, n)


E2M1 = np.array([0.0, 0.5, 1.0, 1.5, 2.0, 3.0, 4.0, 6.0, -0.0, -0.5, -1.0, -1.5, -2.0, -3.0, -4.0, -6.0])


def pack_fp4(w):
    k, n = w.shape
    w = f64(np.asarray(w, np.float32).astype(ml_dtypes.bfloat16)).reshape(k // 32, 32, n)
    amax = np.abs(w).max(1)
    mant, ex = np.frexp(amax / 6.0)
    byte = np.clip(np.where(amax > 0, np.where(mant > 0.5, ex, ex - 1) + 127, 1), 1, 254)
    scaled = (w * np.exp2(127.0 - byte)[:, None, :]).reshape(k, n).astype(np.float32)
    c = np.ascontiguousarray(scaled.reshape(k // 512, 128, 4, n).transpose(0, 1, 3, 2)).astype(ml_dtypes.float4_e2m1fn).view(np.uint8) & 0xF
    words = (c[..., 0::2] | (c[..., 1::2] << 4)).reshape(k // 512, 128, 2 * n)
    return np.ascontiguousarray(words), np.ascontiguousarray(byte.astype(np.uint8).reshape(k // 512, 16, n))


def unpack_fp4(words, scales):
    g, _, n = scales.shape
    words = np.ascontiguousarray(words).reshape(g, 128, n, 2)
    nib = np.empty((g, 128, n, 4), np.uint8)
    nib[..., 0::2] = words & 0xF
    nib[..., 1::2] = words >> 4
    vals = E2M1[nib] * np.repeat(np.exp2(scales.astype(np.float64) - 127.0), 8, axis=1)[..., None]
    return vals.transpose(0, 1, 3, 2).reshape(g * 512, n)


def sigmoid(v):
    return 1.0 / (1.0 + np.exp(-np.maximum(v, -700.0)))

def planes(y):
    n, m = y.shape
    v = y.astype(np.float32).astype(ml_dtypes.bfloat16).astype(np.float64).reshape(n // 32, 32, m)
    top = np.abs(v).max(1)
    byte = np.clip(np.where(top > 0, np.frexp(top)[1] - 1 + 127 - 7, 1), 1, 254)
    codes = (v * np.exp2(127.0 - byte)[:, None, :]).reshape(n, m).astype(np.float32).astype(ml_dtypes.float8_e4m3fn).view(np.uint8)
    words = codes.reshape(n // 512, 128, 4, m).transpose(0, 1, 3, 2)
    return np.ascontiguousarray(words), np.ascontiguousarray(byte.astype(np.uint8).reshape(n // 512, 16, m))


K, T, S, N, G, H, W, U = 512, 1024, 512, 512, 2048, 512, 1024, 384


def setup_inputs():
    n = np.random.standard_normal
    s = mx_kscale(K)[:, None]
    u = mx_kscale(S)
    packed_xT = pack_weight(n((K, T)) * s)
    packed_dT = pack_weight(n((K, G)) / s)
    packed_w1 = pack_fp4(n((H, N)) / np.sqrt(2 * H) / u[:, None])
    packed_w2 = pack_fp4(n((H, N)) / np.sqrt(2 * H) / u[:, None])
    return {
        "x_words": packed_xT[0],
        "x_scales": packed_xT[1],
        "d_words": packed_dT[0],
        "d_scales": packed_dT[1],
        "gn": (np.random.uniform(0.5, 1.5, (H, 1)) * u[:, None]).astype(np.float32),
        "gm": (np.random.uniform(0.5, 1.5, (H, 1)) * u[:, None]).astype(np.float32),
        "w1_words": packed_w1[0],
        "w1_scales": packed_w1[1],
        "w2_words": packed_w2[0],
        "w2_scales": packed_w2[1],
        "offs": striped(np.random.permutation(T)[:S]),
        "k1": striped8(np.random.randint(0, G, (8, H))),
        "two": striped(np.random.permutation(T)[:S]),
        "k2": striped8(np.random.randint(0, G, (8, H))),
        "n1": striped8(np.stack([np.random.permutation(S) for _ in range(8)])),
        "n2": striped8(np.stack([np.random.permutation(S) for _ in range(8)])),
        "n3": striped(np.random.randint(0, S, W)),
        "n4": striped(np.random.permutation(S)[:U]),
        "n5": striped(np.random.permutation(S)[:U]),
    }


def reference(x_words, x_scales, d_words, d_scales, gn, gm, w1_words, w1_scales, w2_words, w2_scales, offs, k1, two, k2, n1, n2, n3, n4, n5):
    d_k1 = unpack_weight(d_words, d_scales)[np.arange(K)[:, None], runs(k1, K)]
    xq = unpack_weight(x_words, x_scales)[:, unstriped(offs)]
    a = 0.0625 * (d_k1.T @ xq)
    ex = np.exp(0.5 * a)
    z = f64(gn) * ((2.0 * ex) / (ex + ex[np.arange(H)[:, None], runs(n1, H)] + ex[np.arange(H)[:, None], runs(n2, H)]))
    d_k2 = unpack_weight(d_words, d_scales)[np.arange(K)[:, None], runs(k2, K)]
    x_two = unpack_weight(x_words, x_scales)[:, unstriped(two)]
    b = 0.0625 * (d_k2.T @ x_two)
    mb = b[:, unstriped(n3)]
    mn = mb.reshape(H, S, 2).min(axis=2)
    mx = mb.reshape(H, S, 2).max(axis=2)
    z2 = f64(gm) * ((b - mn) * sigmoid(mx))
    h = unpack_fp4(w1_words, w1_scales).T @ mxq(z, 0, "e4m3") + unpack_fp4(w2_words, w2_scales).T @ mxq(z2, 0, "e4m3")
    pa = h[:, unstriped(n5)]
    old = h[:, unstriped(n4)]
    ra = np.maximum(pa, 0.5 * old)
    out = h.copy()
    out[:, unstriped(n4)] = ra
    return (out,) + planes(out)

@@ -1,0 +1,298 @@
+from contextlib import ExitStack
+
+import concourse.mybir as mybir
+from concourse.masks import make_identity
+
+F32 = mybir.dt.float32
+BF16 = mybir.dt.bfloat16
+I32 = mybir.dt.int32
+U32 = mybir.dt.uint32
+U16 = mybir.dt.uint16
+U8 = mybir.dt.uint8
+FP8X4 = mybir.dt.float8_e4m3fn_x4
+FP4X4 = mybir.dt.float4_e2m1fn_x4
+ACT = mybir.ActivationFunctionType
+ALU = mybir.AluOpType
+
+P = 128
+PACK = 4
+S = 512
+T = 1024
+G = 2048
+U = 384
+HALF = 256
+FLOPS = 4 * 2 * 512 * 512 * 512
+
+
+def tile_picked_pqjshareghardkmax_none_po_kernel(
+    tc, x_words, x_scales, d_words, d_scales, gn, gm, w1_words, w1_scales, w2_words, w2_scales,
+    offs, k1, two, k2, n1, n2, n3, n4, n5, out_0, out_1, out_2,
+):
+    nc = tc.nc
+    with ExitStack() as ctx:
+        keep = ctx.enter_context(tc.tile_pool(name="keep", bufs=1))
+        ring = ctx.enter_context(tc.tile_pool(name="ring", bufs=2))
+        mm = ctx.enter_context(tc.psum_pool(name="mm", bufs=4))
+        turn = ctx.enter_context(tc.psum_pool(name="turn", bufs=2))
+
+        def load_list(src, name):
+            tile = keep.tile(list(src.shape), U16, name=name)
+            nc.sync.dma_start(tile[:], src)
+            return tile
+
+        def cols(lst, start, count):
+            return lst[:, start // 16 : (start + count) // 16]
+
+        k1_list = load_list(k1, "k1_list")
+        d_byte_table = keep.tile([P, G], U8, name="d_byte_table")
+        d_rows = d_scales[0].bitcast(I32).rearrange("(r e) c -> e r c", e=2)
+        for e in range(2):
+            nc.sync.dma_start(d_byte_table[e:P:2, :].bitcast(I32), d_rows[e].unsqueeze(1).to_broadcast([8, 8, G // 4]))
+        offs_list = load_list(offs, "offs_list")
+
+        def load_plane(dst, scales, width):
+            rows = scales[0].bitcast(I32).rearrange("(q r) c -> r q c", r=4)
+            for r in range(4):
+                nc.sync.dma_start(dst[r:P:4, :].bitcast(I32), rows[r].unsqueeze(1).to_broadcast([4, 8, width // 4]))
+
+        x_byte_table = keep.tile([P, T], U8, name="x_byte_table", tag="byte_rows")
+        load_plane(x_byte_table, x_scales, T)
+        d_word_table = keep.tile([P, G], U32, name="d_word_table")
+        nc.sync.dma_start(d_word_table[:].bitcast(I32), d_words[0].rearrange("p n t -> p (n t)").bitcast(I32))
+        x_word_table = keep.tile([P, T], U32, name="x_word_table")
+        nc.sync.dma_start(x_word_table[:].bitcast(I32), x_words[0].rearrange("p n t -> p (n t)").bitcast(I32))
+
+        ident = keep.tile([P, P], F32, name="ident")
+        make_identity(nc, ident[:])
+
+        def first_product(d_list, x_list, name):
+            d_bytes = keep.tile([P, S], U8, name=name + "_d_bytes", tag=name + "_small")
+            nc.vector.tensor_copy(d_bytes[:], d_byte_table[:].indirect(d_list[:]))
+            d_plane = keep.tile([P, S], U8, name=name + "_d_plane", align_bytes=64)
+            nc.vector.tensor_copy(
+                d_plane[:].rearrange("p (t c i) -> p c t i", t=PACK, i=16),
+                d_bytes[:].rearrange("p (c i t) -> p c t i", t=PACK, i=16),
+            )
+            for e in range(2):
+                nc.sync.dma_start(d_plane[2 + e : P : 32, :].bitcast(I32), d_plane[16 + e : P : 32, :].bitcast(I32))
+            x_plane = keep.tile([P, S], U8, name=name + "_x_plane", align_bytes=64)
+            nc.vector.tensor_copy(x_plane[:], x_byte_table[:].indirect(x_list[:]))
+            d_picked = keep.tile([P, S], U32, name=name + "_d_picked", tag=name + "_picked")
+            nc.vector.tensor_copy(d_picked[:], d_word_table[:].indirect(d_list[:]))
+            d_codes = keep.tile([P, S], U32, name=name + "_d_codes", align_bytes=64)
+            nc.vector.tensor_copy(
+                d_codes[:].rearrange("p (t c i) -> p c t i", t=PACK, i=4),
+                d_picked[:].rearrange("p (c i t) -> p c t i", t=PACK, i=4),
+            )
+            x_codes = keep.tile([P, S], U32, name=name + "_x_codes", align_bytes=64)
+            nc.vector.tensor_copy(x_codes[:], x_word_table[:].indirect(x_list[:]))
+            banks = []
+            for t in range(PACK):
+                bank = mm.tile([P, S], F32, name="bank")
+                m_cols = slice(t * P, (t + 1) * P)
+                nc.tensor.matmul_mx(
+                    bank[:], lhsT=d_codes[:, m_cols].bitcast(FP8X4), lhsT_scale=d_plane[:, m_cols],
+                    rhs=x_codes[:].bitcast(FP8X4), rhs_scale=x_plane[:], start=True, stop=True,
+                )
+                banks.append(bank)
+            return banks
+
+        def gather(engine, out, window, offsets):
+            if engine == "vector":
+                nc.vector.tensor_copy(out, window[:].indirect(offsets))
+            else:
+                nc.scalar.activation(out, window[:].indirect(offsets), ACT.Copy)
+
+        def interleave(engine, grouped, planes, lo, hi):
+            dst = grouped[:, lo:hi, :].rearrange("p (c i) t -> p c t i", i=4)
+            src = planes[:, :, lo:hi].rearrange("p t (c i) -> p c t i", i=4)
+            if engine == "vector":
+                nc.vector.tensor_copy(dst, src)
+            else:
+                nc.scalar.copy(dst, src)
+
+        def quantize(codes, plane, grouped, lo, hi):
+            nc.vector.quantize_mx(
+                codes[:, lo:hi].bitcast(FP8X4), plane[:, lo:hi], grouped[:, lo:hi, :].rearrange("p j t -> p (j t)")
+            )
+
+        def mx_tiles(name):
+            grouped = keep.tile([P, S, PACK], BF16, name=name + "_grouped", align_bytes=64)
+            codes = keep.tile([P, S], U32, name=name + "_codes", align_bytes=64)
+            plane = keep.tile([P, S], U8, name=name + "_plane", align_bytes=64)
+            return grouped, codes, plane
+
+        def gather_halves(engine, out, window, lst, count):
+            for start in range(0, count, HALF):
+                gather(engine, out[:, start : start + HALF], window, cols(lst, start, HALF))
+
+        a_banks = first_product(k1_list, offs_list, "a")
+        k2_list = load_list(k2, "k2_list")
+        two_list = load_list(two, "two_list")
+        n1_list = load_list(n1, "n1_list")
+        n2_list = load_list(n2, "n2_list")
+        ex = []
+        for t in range(PACK):
+            ex_t = keep.tile([P, S], F32, name="ex%d" % t)
+            nc.scalar.activation(ex_t[:], a_banks[t][:], ACT.Exp, scale=0.03125)
+            ex.append(ex_t)
+
+        b_banks = first_product(k2_list, two_list, "b")
+        n3_list = load_list(n3, "n3_list")
+        n4_list = load_list(n4, "n4_list")
+        n5_list = load_list(n5, "n5_list")
+        gains = keep.tile([P, 2, 8], F32, name="gains", tag="a_small")
+        gn_rows = gains[:, 0, 0:PACK]
+        nc.sync.dma_start(gn_rows[:], gn.rearrange("(p t) o -> p (t o)", t=PACK))
+        gm_rows = gains[:, 1, 0:PACK]
+        nc.sync.dma_start(gm_rows[:], gm.rearrange("(p t) o -> p (t o)", t=PACK))
+        w_bytes = keep.tile([P, 2, S], U8, name="w_bytes", tag="b_small")
+        w_raw = keep.tile([P, 2, 2 * S], U8, name="w_raw", tag="b_picked")
+        for w, words in enumerate((w1_words, w2_words)):
+            nc.sync.dma_start(w_raw[:, w, :].bitcast(I32), words[0].bitcast(I32))
+        for w, scales in enumerate((w1_scales, w2_scales)):
+            load_plane(w_bytes[:, w, :], scales, S)
+
+        looked = [keep.tile([P, 2, S], F32, name="ex_looked%d" % t) for t in range(PACK)]
+        b = [keep.tile([P, S], F32, name="b%d" % t) for t in range(PACK)]
+        mb = [keep.tile([P, S, 2], F32, name="mb%d" % t, align_bytes=64) for t in range(PACK)]
+        high = keep.tile([P, PACK, S], F32, name="high", align_bytes=64)
+        gap = keep.tile([P, PACK, S], F32, name="gap")
+        gate = keep.tile([P, PACK, S], F32, name="gate")
+        z_planes = keep.tile([P, PACK, S], BF16, name="z_planes")
+        z2_planes = keep.tile([P, PACK, S], BF16, name="z2_planes")
+
+        def look_up_ex(engine, t):
+            for n, lst in enumerate((n1_list, n2_list)):
+                gather_halves(engine, looked[t][:, n, :], ex[t], lst, S)
+
+        def look_up_b(engine, t):
+            gather_halves(engine, mb[t][:].rearrange("p j e -> p (j e)"), b[t], n3_list, 2 * S)
+
+        def members(t):
+            nc.vector.tensor_tensor(high[:, t, :], mb[t][:, :, 0], mb[t][:, :, 1], ALU.max)
+            low = ring.tile([P, S], F32, name="low")
+            nc.vector.tensor_tensor(low[:], mb[t][:, :, 0], mb[t][:, :, 1], ALU.min)
+            nc.vector.tensor_tensor(gap[:, t, :], b[t][:], low[:], ALU.subtract)
+
+        def share(t):
+            den = mm.tile([P, S], F32, name="bank")
+            for c in range(PACK):
+                blk = slice(c * P, (c + 1) * P)
+                terms = (ex[t][:, blk], looked[t][:, 0, blk], looked[t][:, 1, blk])
+                for n, term in enumerate(terms):
+                    nc.tensor.matmul(den[:, blk], term, ident[:], start=(n == 0), stop=(n == 2), is_transpose=True)
+            root = gate[:, :, t * P : (t + 1) * P] if t < 3 else gate[:, :, :].rearrange("p t (h j) -> p (t h) j", h=2)[:, :, 0:64]
+            width = root.shape[2]
+            nc.scalar.activation(root, den[:].rearrange("p (c j) -> p c j", j=width), ACT.Abs_reciprocal_sqrt, scale=0.5)
+            inv = ring.tile([P, S], F32, name="inv")
+            nc.scalar.activation(inv[:].rearrange("p (c j) -> p c j", j=width), root, ACT.Square)
+            back = turn.tile([P, S], F32, name="back", bufs=4)
+            for c in range(PACK):
+                blk = slice(c * P, (c + 1) * P)
+                nc.tensor.transpose(back[:, blk], inv[:, blk], ident[:])
+            nc.vector.scalar_tensor_tensor(z_planes[:, t, :], back[:], gn_rows[:, t : t + 1], ex[t][:], ALU.mult, ALU.mult)
+
+        look_up_ex("vector", 0)
+        look_up_ex("scalar", 1)
+        look_up_ex("scalar", 2)
+        for t in range(2):
+            nc.vector.tensor_scalar(b[t][:], b_banks[t][:], 0.0625, None, ALU.mult)
+        look_up_ex("scalar", 3)
+        for t in range(2, PACK):
+            nc.scalar.activation(b[t][:], b_banks[t][:], ACT.Copy, scale=0.0625)
+        look_up_b("vector", 0)
+        members(0)
+        look_up_b("scalar", 2)
+        look_up_b("vector", 1)
+        members(1)
+        look_up_b("scalar", 3)
+        members(2)
+        members(3)
+        w_planes = keep.tile([P, 2, S], U8, name="w_planes", tag="mb3", align_bytes=64)
+        for w in range(2):
+            nc.vector.tensor_copy(
+                w_planes[:, w, :].rearrange("p (t c i) -> p c t i", t=PACK, i=16),
+                w_bytes[:, w, :].rearrange("p (c i t) -> p c t i", t=PACK, i=16),
+            )
+        for t in range(PACK):
+            share(t)
+        z_grouped, z_codes, z_plane = mx_tiles("z")
+        interleave("vector", z_grouped, z_planes, 0, S)
+        quantize(z_codes, z_plane, z_grouped, 0, S)
+
+        for half in range(2):
+            lo, hi = half * HALF, (half + 1) * HALF
+            nc.scalar.activation(gate[:, :, lo:hi], high[:, :, lo:hi], ACT.Sigmoid)
+        w_codes = keep.tile([P, 2, 2 * S], U8, name="w_codes", tag="high", align_bytes=64)
+        for w in range(2):
+            nc.scalar.copy(
+                w_codes[:, w, :].bitcast(U16).rearrange("p (t c i) -> p c t i", t=PACK, i=8),
+                w_raw[:, w, :].bitcast(U16).rearrange("p (c i t) -> p c t i", t=PACK, i=8),
+            )
+
+        def second_product(bank, t, w, codes, plane, lo):
+            nc.tensor.matmul_mx(
+                bank[:], lhsT=w_codes[:, w, 2 * t * P : 2 * (t + 1) * P].bitcast(FP4X4),
+                lhsT_scale=w_planes[:, w, t * P : (t + 1) * P],
+                rhs=codes[:, lo : lo + HALF].bitcast(FP8X4), rhs_scale=plane[:, lo : lo + HALF],
+                start=(w == 0), stop=(w == 1),
+            )
+
+        h_banks = [
+            [turn.tile([P, HALF], F32, name="back", bufs=4) for t in range(PACK)],
+            [mm.tile([P, HALF], F32, name="bank") for t in range(PACK)],
+        ]
+        for half in range(2):
+            for t in range(PACK):
+                second_product(h_banks[half][t], t, 0, z_codes, z_plane, half * HALF)
+
+        z2_grouped, z2_codes, z2_plane = mx_tiles("z2")
+        h = [keep.tile([P, S], F32, name="h%d" % t) for t in range(PACK)]
+        for half in range(2):
+            lo, hi = half * HALF, (half + 1) * HALF
+            for t in range(PACK):
+                nc.vector.scalar_tensor_tensor(
+                    z2_planes[:, t, lo:hi], gap[:, t, lo:hi], gm_rows[:, t : t + 1], gate[:, t, lo:hi], ALU.mult, ALU.mult
+                )
+            interleave("vector" if half else "scalar", z2_grouped, z2_planes, lo, hi)
+        for half in range(2):
+            lo, hi = half * HALF, (half + 1) * HALF
+            quantize(z2_codes, z2_plane, z2_grouped, lo, hi)
+            for t in range(PACK):
+                second_product(h_banks[half][t], t, 1, z2_codes, z2_plane, lo)
+            for t in range(PACK):
+                if half == 1 and t % 2 == 0:
+                    nc.vector.tensor_copy(h[t][:, lo:hi], h_banks[half][t][:])
+                else:
+                    nc.scalar.copy(h[t][:, lo:hi], h_banks[half][t][:])
+
+        out_rows = out_0.rearrange("(p t) j -> p t j", t=PACK)
+        y_planes = keep.tile([P, PACK, S], BF16, name="y_planes")
+        pa = [keep.tile([P, 2, U], F32, name="pa%d" % e) for e in range(2)]
+        old = [keep.tile([P, 2, U], F32, name="old%d" % e) for e in range(2)]
+        for t in range(PACK):
+            engine = "scalar" if t % 2 else "vector"
+            gather(engine, pa[t % 2][:, t // 2, :], h[t], n5_list[:])
+            gather(engine, old[t % 2][:, t // 2, :], h[t], n4_list[:])
+        ra_odd = keep.tile([P, 2, U], F32, name="ra_odd")
+        nc.vector.scalar_tensor_tensor(ra_odd[:], old[1][:], 0.5, pa[1][:], ALU.mult, ALU.max)
+        ra_even = keep.tile([P, 2, U], F32, name="ra_even", tag="pa1")
+        nc.vector.scalar_tensor_tensor(ra_even[:], old[0][:], 0.5, pa[0][:], ALU.mult, ALU.max)
+        for t in range(PACK):
+            if t % 2:
+                nc.scalar.activation(h[t][:].indirect(n4_list[:]), ra_odd[:, t // 2, :], ACT.Copy)
+            else:
+                nc.vector.tensor_copy(h[t][:].indirect(n4_list[:]), ra_even[:, t // 2, :])
+            nc.sync.dma_start(out_rows[:, t, :], h[t][:])
+        for t in range(PACK):
+            if t % 2:
+                nc.scalar.copy(y_planes[:, t, :], h[t][:])
+            else:
+                nc.vector.tensor_copy(y_planes[:, t, :], h[t][:])
+        y_grouped, y_codes, y_plane = mx_tiles("y")
+        interleave("vector", y_grouped, y_planes, 0, S)
+        quantize(y_codes, y_plane, y_grouped, 0, S)
+        nc.sync.dma_start(out_1[0].rearrange("p n t -> p (n t)").bitcast(I32), y_codes[:].bitcast(I32))
+        for q in range(4):
+            nc.scalar.dma_start(out_2[0, 4 * q : 4 * q + 4, :].bitcast(I32), y_plane[32 * q : 32 * q + 4, :].bitcast(I32))

@@ -21,6 +21,8 @@ T = 1024
 G = 2048
 U = 384
 HALF = 256
+B_WIDTH = 544
+SCALAR_SHARE = 160
 FLOPS = 4 * 2 * 512 * 512 * 512
 
 
@@ -31,6 +33,7 @@ def tile_picked_pqjshareghardkmax_none_po_kernel(
     nc = tc.nc
     with ExitStack() as ctx:
         keep = ctx.enter_context(tc.tile_pool(name="keep", bufs=1))
+        picked = ctx.enter_context(tc.tile_pool(name="picked", bufs=1))
         ring = ctx.enter_context(tc.tile_pool(name="ring", bufs=2))
         mm = ctx.enter_context(tc.psum_pool(name="mm", bufs=4))
         turn = ctx.enter_context(tc.psum_pool(name="turn", bufs=2))
@@ -50,23 +53,26 @@ def tile_picked_pqjshareghardkmax_none_po_kernel(
             nc.sync.dma_start(d_byte_table[e:P:2, :].bitcast(I32), d_rows[e].unsqueeze(1).to_broadcast([8, 8, G // 4]))
         offs_list = load_list(offs, "offs_list")
 
-        def load_plane(dst, scales, width):
+        def load_plane(dst, scales, width, which):
             rows = scales[0].bitcast(I32).rearrange("(q r) c -> r q c", r=4)
-            for r in range(4):
+            for r in which:
                 nc.sync.dma_start(dst[r:P:4, :].bitcast(I32), rows[r].unsqueeze(1).to_broadcast([4, 8, width // 4]))
 
-        x_byte_table = keep.tile([P, T], U8, name="x_byte_table", tag="byte_rows")
-        load_plane(x_byte_table, x_scales, T)
-        d_word_table = keep.tile([P, G], U32, name="d_word_table")
-        nc.sync.dma_start(d_word_table[:].bitcast(I32), d_words[0].rearrange("p n t -> p (n t)").bitcast(I32))
+        x_byte_table = keep.tile([P, T], U8, name="x_byte_table")
+        load_plane(x_byte_table, x_scales, T, range(3))
         x_word_table = keep.tile([P, T], U32, name="x_word_table")
         nc.sync.dma_start(x_word_table[:].bitcast(I32), x_words[0].rearrange("p n t -> p (n t)").bitcast(I32))
+        load_plane(x_byte_table, x_scales, T, range(3, 4))
+        k2_list = load_list(k2, "k2_list")
+        two_list = load_list(two, "two_list")
+        d_word_table = keep.tile([P, G], U32, name="d_word_table")
+        nc.sync.dma_start(d_word_table[:].bitcast(I32), d_words[0].rearrange("p n t -> p (n t)").bitcast(I32))
 
         ident = keep.tile([P, P], F32, name="ident")
         make_identity(nc, ident[:])
 
-        def first_product(d_list, x_list, name):
-            d_bytes = keep.tile([P, S], U8, name=name + "_d_bytes", tag=name + "_small")
+        def first_product(d_list, x_list, name, place):
+            d_bytes = picked.tile([P, S], U8, name=name + "_d_bytes", align_bytes=64, offset=place["d_bytes"])
             nc.vector.tensor_copy(d_bytes[:], d_byte_table[:].indirect(d_list[:]))
             d_plane = keep.tile([P, S], U8, name=name + "_d_plane", align_bytes=64)
             nc.vector.tensor_copy(
@@ -75,17 +81,17 @@ def tile_picked_pqjshareghardkmax_none_po_kernel(
             )
             for e in range(2):
                 nc.sync.dma_start(d_plane[2 + e : P : 32, :].bitcast(I32), d_plane[16 + e : P : 32, :].bitcast(I32))
-            x_plane = keep.tile([P, S], U8, name=name + "_x_plane", align_bytes=64)
+            x_codes = picked.tile([P, S], U32, name=name + "_x_codes", align_bytes=64, offset=place["x_codes"])
+            nc.vector.tensor_copy(x_codes[:], x_word_table[:].indirect(x_list[:]))
+            x_plane = picked.tile([P, S], U8, name=name + "_x_plane", align_bytes=64, offset=place["x_plane"])
             nc.vector.tensor_copy(x_plane[:], x_byte_table[:].indirect(x_list[:]))
-            d_picked = keep.tile([P, S], U32, name=name + "_d_picked", tag=name + "_picked")
+            d_picked = picked.tile([P, S], U32, name=name + "_d_picked", align_bytes=64, offset=place["d_picked"])
             nc.vector.tensor_copy(d_picked[:], d_word_table[:].indirect(d_list[:]))
             d_codes = keep.tile([P, S], U32, name=name + "_d_codes", align_bytes=64)
             nc.vector.tensor_copy(
                 d_codes[:].rearrange("p (t c i) -> p c t i", t=PACK, i=4),
                 d_picked[:].rearrange("p (c i t) -> p c t i", t=PACK, i=4),
             )
-            x_codes = keep.tile([P, S], U32, name=name + "_x_codes", align_bytes=64)
-            nc.vector.tensor_copy(x_codes[:], x_word_table[:].indirect(x_list[:]))
             banks = []
             for t in range(PACK):
                 bank = mm.tile([P, S], F32, name="bank")
@@ -122,39 +128,39 @@ def tile_picked_pqjshareghardkmax_none_po_kernel(
             plane = keep.tile([P, S], U8, name=name + "_plane", align_bytes=64)
             return grouped, codes, plane
 
-        def gather_halves(engine, out, window, lst, count):
-            for start in range(0, count, HALF):
-                gather(engine, out[:, start : start + HALF], window, cols(lst, start, HALF))
-
-        a_banks = first_product(k1_list, offs_list, "a")
-        k2_list = load_list(k2, "k2_list")
-        two_list = load_list(two, "two_list")
+        a_banks = first_product(k1_list, offs_list, "a", {"d_picked": 2048, "d_bytes": 5184, "x_plane": 5696, "x_codes": 6208})
         n1_list = load_list(n1, "n1_list")
         n2_list = load_list(n2, "n2_list")
         ex = []
+        ex_window = []
         for t in range(PACK):
-            ex_t = keep.tile([P, S], F32, name="ex%d" % t)
-            nc.scalar.activation(ex_t[:], a_banks[t][:], ACT.Exp, scale=0.03125)
-            ex.append(ex_t)
+            window = keep.tile([P, 2 * S], F32, name="ex%d" % t)
+            (nc.gpsimd if t % 2 else nc.vector).memset(window[:, S:], 0.0)
+            nc.scalar.activation(window[:, 0:S], a_banks[t][:], ACT.Exp, scale=0.03125)
+            ex_window.append(window)
+            ex.append(window[:, 0:S])
 
-        b_banks = first_product(k2_list, two_list, "b")
+        b_banks = first_product(k2_list, two_list, "b", {"d_picked": 64, "d_bytes": 2112, "x_plane": 2624, "x_codes": 3136})
         n3_list = load_list(n3, "n3_list")
         n4_list = load_list(n4, "n4_list")
         n5_list = load_list(n5, "n5_list")
-        gains = keep.tile([P, 2, 8], F32, name="gains", tag="a_small")
+        gains = picked.tile([P, 2, 8], F32, name="gains", align_bytes=64, offset=5184)
         gn_rows = gains[:, 0, 0:PACK]
         nc.sync.dma_start(gn_rows[:], gn.rearrange("(p t) o -> p (t o)", t=PACK))
         gm_rows = gains[:, 1, 0:PACK]
         nc.sync.dma_start(gm_rows[:], gm.rearrange("(p t) o -> p (t o)", t=PACK))
-        w_bytes = keep.tile([P, 2, S], U8, name="w_bytes", tag="b_small")
-        w_raw = keep.tile([P, 2, 2 * S], U8, name="w_raw", tag="b_picked")
+        w_bytes = picked.tile([P, 2, S], U8, name="w_bytes", align_bytes=64, offset=5696)
+        w_raw = picked.tile([P, 2, 2 * S], U8, name="w_raw", align_bytes=64, offset=0)
         for w, words in enumerate((w1_words, w2_words)):
             nc.sync.dma_start(w_raw[:, w, :].bitcast(I32), words[0].bitcast(I32))
         for w, scales in enumerate((w1_scales, w2_scales)):
-            load_plane(w_bytes[:, w, :], scales, S)
+            load_plane(w_bytes[:, w, :], scales, S, range(4))
 
         looked = [keep.tile([P, 2, S], F32, name="ex_looked%d" % t) for t in range(PACK)]
-        b = [keep.tile([P, S], F32, name="b%d" % t) for t in range(PACK)]
+        b_window = [keep.tile([P, B_WIDTH], F32, name="b%d" % t) for t in range(PACK)]
+        for window in b_window:
+            nc.gpsimd.memset(window[:, S:], 0.0)
+        b = [window[:, 0:S] for window in b_window]
         mb = [keep.tile([P, S, 2], F32, name="mb%d" % t, align_bytes=64) for t in range(PACK)]
         high = keep.tile([P, PACK, S], F32, name="high", align_bytes=64)
         gap = keep.tile([P, PACK, S], F32, name="gap")
@@ -164,10 +170,12 @@ def tile_picked_pqjshareghardkmax_none_po_kernel(
 
         def look_up_ex(engine, t):
             for n, lst in enumerate((n1_list, n2_list)):
-                gather_halves(engine, looked[t][:, n, :], ex[t], lst, S)
+                gather(engine, looked[t][:, n, :], ex_window[t], lst[:])
 
         def look_up_b(engine, t):
-            gather_halves(engine, mb[t][:].rearrange("p j e -> p (j e)"), b[t], n3_list, 2 * S)
+            flat = mb[t][:].rearrange("p j e -> p (j e)")
+            for start in (0, S):
+                gather(engine, flat[:, start : start + S], b_window[t], cols(n3_list, start, S))
 
         def members(t):
             nc.vector.tensor_tensor(high[:, t, :], mb[t][:, :, 0], mb[t][:, :, 1], ALU.max)
@@ -182,16 +190,17 @@ def tile_picked_pqjshareghardkmax_none_po_kernel(
                 terms = (ex[t][:, blk], looked[t][:, 0, blk], looked[t][:, 1, blk])
                 for n, term in enumerate(terms):
                     nc.tensor.matmul(den[:, blk], term, ident[:], start=(n == 0), stop=(n == 2), is_transpose=True)
-            root = gate[:, :, t * P : (t + 1) * P] if t < 3 else gate[:, :, :].rearrange("p t (h j) -> p (t h) j", h=2)[:, :, 0:64]
-            width = root.shape[2]
-            nc.scalar.activation(root, den[:].rearrange("p (c j) -> p c j", j=width), ACT.Abs_reciprocal_sqrt, scale=0.5)
-            inv = ring.tile([P, S], F32, name="inv")
-            nc.scalar.activation(inv[:].rearrange("p (c j) -> p c j", j=width), root, ACT.Square)
+            root = ring.tile([P, PACK, P], F32, name="root", bufs=4)
+            nc.scalar.activation(root[:], den[:].rearrange("p (c j) -> p c j", j=P), ACT.Abs_reciprocal_sqrt, scale=0.5)
             back = turn.tile([P, S], F32, name="back", bufs=4)
             for c in range(PACK):
-                blk = slice(c * P, (c + 1) * P)
-                nc.tensor.transpose(back[:, blk], inv[:, blk], ident[:])
-            nc.vector.scalar_tensor_tensor(z_planes[:, t, :], back[:], gn_rows[:, t : t + 1], ex[t][:], ALU.mult, ALU.mult)
+                nc.tensor.transpose(back[:, c * P : (c + 1) * P], root[:, c, :], ident[:])
+            return back
+
+        def weigh(t, back):
+            inv = gate[:].rearrange("p t (h j) -> p (t h) j", h=2)[:, :, t * 64 : (t + 1) * 64]
+            nc.scalar.activation(inv, back[:].rearrange("p (c j) -> p c j", j=64), ACT.Square)
+            nc.vector.scalar_tensor_tensor(z_planes[:, t, :].rearrange("p (c j) -> p c j", j=64), inv, gn_rows[:, t : t + 1], ex[t][:].rearrange("p (c j) -> p c j", j=64), ALU.mult, ALU.mult)
 
         look_up_ex("vector", 0)
         look_up_ex("scalar", 1)
@@ -206,34 +215,42 @@ def tile_picked_pqjshareghardkmax_none_po_kernel(
         look_up_b("scalar", 2)
         look_up_b("vector", 1)
         members(1)
-        look_up_b("scalar", 3)
         members(2)
-        members(3)
-        w_planes = keep.tile([P, 2, S], U8, name="w_planes", tag="mb3", align_bytes=64)
+        w_planes = keep.tile([P, 2, S], U8, name="w_planes", tag="mb2", align_bytes=64)
         for w in range(2):
             nc.vector.tensor_copy(
                 w_planes[:, w, :].rearrange("p (t c i) -> p c t i", t=PACK, i=16),
                 w_bytes[:, w, :].rearrange("p (c i t) -> p c t i", t=PACK, i=16),
             )
+        backs = [share(t) for t in range(PACK)]
         for t in range(PACK):
-            share(t)
+            weigh(t, backs[t])
+        look_up_b("scalar", 3)
+        w_codes = []
+
+        def deal_weights(w, tag):
+            dealt = keep.tile([P, 2 * S], U8, name="w_codes%d" % w, tag=tag, align_bytes=64)
+            nc.scalar.copy(
+                dealt[:].bitcast(U16).rearrange("p (t c i) -> p c t i", t=PACK, i=8),
+                w_raw[:, w, :].bitcast(U16).rearrange("p (c i t) -> p c t i", t=PACK, i=8),
+            )
+            w_codes.append(dealt)
+
+        deal_weights(0, "w_codes0")
         z_grouped, z_codes, z_plane = mx_tiles("z")
         interleave("vector", z_grouped, z_planes, 0, S)
         quantize(z_codes, z_plane, z_grouped, 0, S)
+        members(3)
 
         for half in range(2):
             lo, hi = half * HALF, (half + 1) * HALF
-            nc.scalar.activation(gate[:, :, lo:hi], high[:, :, lo:hi], ACT.Sigmoid)
-        w_codes = keep.tile([P, 2, 2 * S], U8, name="w_codes", tag="high", align_bytes=64)
-        for w in range(2):
-            nc.scalar.copy(
-                w_codes[:, w, :].bitcast(U16).rearrange("p (t c i) -> p c t i", t=PACK, i=8),
-                w_raw[:, w, :].bitcast(U16).rearrange("p (c i t) -> p c t i", t=PACK, i=8),
-            )
+            for t in range(PACK):
+                nc.scalar.activation(gate[:, t, lo:hi], high[:, t, lo:hi], ACT.Sigmoid)
+        deal_weights(1, "high")
 
         def second_product(bank, t, w, codes, plane, lo):
             nc.tensor.matmul_mx(
-                bank[:], lhsT=w_codes[:, w, 2 * t * P : 2 * (t + 1) * P].bitcast(FP4X4),
+                bank[:], lhsT=w_codes[w][:, 2 * t * P : 2 * (t + 1) * P].bitcast(FP4X4),
                 lhsT_scale=w_planes[:, w, t * P : (t + 1) * P],
                 rhs=codes[:, lo : lo + HALF].bitcast(FP8X4), rhs_scale=plane[:, lo : lo + HALF],
                 start=(w == 0), stop=(w == 1),
@@ -255,44 +272,55 @@ def tile_picked_pqjshareghardkmax_none_po_kernel(
                 nc.vector.scalar_tensor_tensor(
                     z2_planes[:, t, lo:hi], gap[:, t, lo:hi], gm_rows[:, t : t + 1], gate[:, t, lo:hi], ALU.mult, ALU.mult
                 )
-            interleave("vector" if half else "scalar", z2_grouped, z2_planes, lo, hi)
-        for half in range(2):
-            lo, hi = half * HALF, (half + 1) * HALF
+            interleave("vector", z2_grouped, z2_planes, lo, hi)
             quantize(z2_codes, z2_plane, z2_grouped, lo, hi)
             for t in range(PACK):
                 second_product(h_banks[half][t], t, 1, z2_codes, z2_plane, lo)
-            for t in range(PACK):
-                if half == 1 and t % 2 == 0:
-                    nc.vector.tensor_copy(h[t][:, lo:hi], h_banks[half][t][:])
-                else:
-                    nc.scalar.copy(h[t][:, lo:hi], h_banks[half][t][:])
+        for t in range(PACK):
+            nc.scalar.copy(h[t][:, 0:HALF], h_banks[0][t][:])
 
         out_rows = out_0.rearrange("(p t) j -> p t j", t=PACK)
         y_planes = keep.tile([P, PACK, S], BF16, name="y_planes")
-        pa = [keep.tile([P, 2, U], F32, name="pa%d" % e) for e in range(2)]
-        old = [keep.tile([P, 2, U], F32, name="old%d" % e) for e in range(2)]
-        for t in range(PACK):
-            engine = "scalar" if t % 2 else "vector"
-            gather(engine, pa[t % 2][:, t // 2, :], h[t], n5_list[:])
-            gather(engine, old[t % 2][:, t // 2, :], h[t], n4_list[:])
+
+        def fetch(engine, t, pa, old):
+            if engine == "vector":
+                nc.vector.tensor_copy(h[t][:, HALF:S], h_banks[1][t][:])
+            else:
+                nc.scalar.copy(h[t][:, HALF:S], h_banks[1][t][:])
+            gather(engine, pa, h[t], n5_list[:])
+            gather(engine, old, h[t], n4_list[:])
+
+        def larger(ra, pa, old):
+            nc.vector.scalar_tensor_tensor(ra, old, 0.5, pa, ALU.mult, ALU.max)
+
+        old_even = keep.tile([P, 2, U], F32, name="old_even")
+        fetched = [keep.tile([P, 2, U], F32, name="fetched%d" % t) for t in (1, 3)]
         ra_odd = keep.tile([P, 2, U], F32, name="ra_odd")
-        nc.vector.scalar_tensor_tensor(ra_odd[:], old[1][:], 0.5, pa[1][:], ALU.mult, ALU.max)
-        ra_even = keep.tile([P, 2, U], F32, name="ra_even", tag="pa1")
-        nc.vector.scalar_tensor_tensor(ra_even[:], old[0][:], 0.5, pa[0][:], ALU.mult, ALU.max)
+        pa0 = keep.tile([P, U], F32, name="pa0")
+        fetch("vector", 0, pa0[:], old_even[:, 0, :])
+        fetch("scalar", 1, fetched[0][:, 0, :], fetched[0][:, 1, :])
+        larger(ra_odd[:, 0, :], fetched[0][:, 0, :], fetched[0][:, 1, :])
+        pa2 = keep.tile([P, U], F32, name="pa2", tag="fetched1")
+        fetch("vector", 2, pa2[:], old_even[:, 1, :])
+        fetch("scalar", 3, fetched[1][:, 0, :], fetched[1][:, 1, :])
+        larger(ra_odd[:, 1, :], fetched[1][:, 0, :], fetched[1][:, 1, :])
+        ra_even = keep.tile([P, 2, U], F32, name="ra_even", tag="fetched3")
+        larger(ra_even[:, 0, :], pa0[:], old_even[:, 0, :])
+        larger(ra_even[:, 1, :], pa2[:], old_even[:, 1, :])
         for t in range(PACK):
             if t % 2:
                 nc.scalar.activation(h[t][:].indirect(n4_list[:]), ra_odd[:, t // 2, :], ACT.Copy)
             else:
                 nc.vector.tensor_copy(h[t][:].indirect(n4_list[:]), ra_even[:, t // 2, :])
             nc.sync.dma_start(out_rows[:, t, :], h[t][:])
-        for t in range(PACK):
-            if t % 2:
-                nc.scalar.copy(y_planes[:, t, :], h[t][:])
-            else:
-                nc.vector.tensor_copy(y_planes[:, t, :], h[t][:])
+        for t in (1, 3, 0):
+            nc.scalar.copy(y_planes[:, t, :], h[t][:])
+        nc.vector.tensor_copy(y_planes[:, 2, :], h[2][:])
         y_grouped, y_codes, y_plane = mx_tiles("y")
-        interleave("vector", y_grouped, y_planes, 0, S)
+        interleave("vector", y_grouped, y_planes, 0, S - SCALAR_SHARE)
+        interleave("scalar", y_grouped, y_planes, S - SCALAR_SHARE, S)
         quantize(y_codes, y_plane, y_grouped, 0, S)
         nc.sync.dma_start(out_1[0].rearrange("p n t -> p (n t)").bitcast(I32), y_codes[:].bitcast(I32))
         for q in range(4):
-            nc.scalar.dma_start(out_2[0, 4 * q : 4 * q + 4, :].bitcast(I32), y_plane[32 * q : 32 * q + 4, :].bitcast(I32))
+            queue = nc.scalar if q % 2 else nc.sync
+            queue.dma_start(out_2[0, 4 * q : 4 * q + 4, :].bitcast(I32), y_plane[32 * q : 32 * q + 4, :].bitcast(I32))

@@ -46,25 +46,25 @@ def tile_picked_pqjshareghardkmax_none_po_kernel(
         def cols(lst, start, count):
             return lst[:, start // 16 : (start + count) // 16]
 
+        def load_plane(dst, scales, width):
+            rows = scales[0].bitcast(I32)
+            for q in range(4):
+                nc.sync.dma_start(
+                    dst[32 * q : 32 * (q + 1), :].bitcast(I32),
+                    rows[4 * q : 4 * q + 4, :].unsqueeze(0).to_broadcast([8, 4, width // 4]),
+                )
+
         k1_list = load_list(k1, "k1_list")
         d_byte_table = keep.tile([P, G], U8, name="d_byte_table")
-        d_rows = d_scales[0].bitcast(I32).rearrange("(r e) c -> e r c", e=2)
-        for e in range(2):
-            nc.sync.dma_start(d_byte_table[e:P:2, :].bitcast(I32), d_rows[e].unsqueeze(1).to_broadcast([8, 8, G // 4]))
+        nc.sync.dma_start(d_byte_table[:].bitcast(I32), d_scales[0].bitcast(I32).unsqueeze(1).to_broadcast([16, 8, G // 4]))
         offs_list = load_list(offs, "offs_list")
-
-        def load_plane(dst, scales, width, which):
-            rows = scales[0].bitcast(I32).rearrange("(q r) c -> r q c", r=4)
-            for r in which:
-                nc.sync.dma_start(dst[r:P:4, :].bitcast(I32), rows[r].unsqueeze(1).to_broadcast([4, 8, width // 4]))
-
         x_byte_table = keep.tile([P, T], U8, name="x_byte_table")
-        load_plane(x_byte_table, x_scales, T, range(3))
+        load_plane(x_byte_table, x_scales, T)
         x_word_table = keep.tile([P, T], U32, name="x_word_table")
         nc.sync.dma_start(x_word_table[:].bitcast(I32), x_words[0].rearrange("p n t -> p (n t)").bitcast(I32))
-        load_plane(x_byte_table, x_scales, T, range(3, 4))
         k2_list = load_list(k2, "k2_list")
         two_list = load_list(two, "two_list")
+        n1_list = load_list(n1, "n1_list")
         d_word_table = keep.tile([P, G], U32, name="d_word_table")
         nc.sync.dma_start(d_word_table[:].bitcast(I32), d_words[0].rearrange("p n t -> p (n t)").bitcast(I32))
 
@@ -79,8 +79,8 @@ def tile_picked_pqjshareghardkmax_none_po_kernel(
                 d_plane[:].rearrange("p (t c i) -> p c t i", t=PACK, i=16),
                 d_bytes[:].rearrange("p (c i t) -> p c t i", t=PACK, i=16),
             )
-            for e in range(2):
-                nc.sync.dma_start(d_plane[2 + e : P : 32, :].bitcast(I32), d_plane[16 + e : P : 32, :].bitcast(I32))
+            for r in range(1, 4):
+                nc.sync.dma_start(d_plane[r:P:32, :].bitcast(I32), d_plane[8 * r : P : 32, :].bitcast(I32))
             x_codes = picked.tile([P, S], U32, name=name + "_x_codes", align_bytes=64, offset=place["x_codes"])
             nc.vector.tensor_copy(x_codes[:], x_word_table[:].indirect(x_list[:]))
             x_plane = picked.tile([P, S], U8, name=name + "_x_plane", align_bytes=64, offset=place["x_plane"])
@@ -129,7 +129,6 @@ def tile_picked_pqjshareghardkmax_none_po_kernel(
             return grouped, codes, plane
 
         a_banks = first_product(k1_list, offs_list, "a", {"d_picked": 2048, "d_bytes": 5184, "x_plane": 5696, "x_codes": 6208})
-        n1_list = load_list(n1, "n1_list")
         n2_list = load_list(n2, "n2_list")
         ex = []
         ex_window = []
@@ -154,7 +153,7 @@ def tile_picked_pqjshareghardkmax_none_po_kernel(
         for w, words in enumerate((w1_words, w2_words)):
             nc.sync.dma_start(w_raw[:, w, :].bitcast(I32), words[0].bitcast(I32))
         for w, scales in enumerate((w1_scales, w2_scales)):
-            load_plane(w_bytes[:, w, :], scales, S, range(4))
+            load_plane(w_bytes[:, w, :], scales, S)
 
         looked = [keep.tile([P, 2, S], F32, name="ex_looked%d" % t) for t in range(PACK)]
         b_window = [keep.tile([P, B_WIDTH], F32, name="b%d" % t) for t in range(PACK)]

@@ -71,7 +71,7 @@ def tile_picked_pqjshareghardkmax_none_po_kernel(
         ident = keep.tile([P, P], F32, name="ident")
         make_identity(nc, ident[:])
 
-        def first_product(d_list, x_list, name, place):
+        def first_product(d_list, x_list, name, place, tokens_first):
             d_bytes = picked.tile([P, S], U8, name=name + "_d_bytes", align_bytes=64, offset=place["d_bytes"])
             nc.vector.tensor_copy(d_bytes[:], d_byte_table[:].indirect(d_list[:]))
             d_plane = keep.tile([P, S], U8, name=name + "_d_plane", align_bytes=64)
@@ -82,16 +82,23 @@ def tile_picked_pqjshareghardkmax_none_po_kernel(
             for r in range(1, 4):
                 nc.sync.dma_start(d_plane[r:P:32, :].bitcast(I32), d_plane[8 * r : P : 32, :].bitcast(I32))
             x_codes = picked.tile([P, S], U32, name=name + "_x_codes", align_bytes=64, offset=place["x_codes"])
-            nc.vector.tensor_copy(x_codes[:], x_word_table[:].indirect(x_list[:]))
             x_plane = picked.tile([P, S], U8, name=name + "_x_plane", align_bytes=64, offset=place["x_plane"])
-            nc.vector.tensor_copy(x_plane[:], x_byte_table[:].indirect(x_list[:]))
             d_picked = picked.tile([P, S], U32, name=name + "_d_picked", align_bytes=64, offset=place["d_picked"])
-            nc.vector.tensor_copy(d_picked[:], d_word_table[:].indirect(d_list[:]))
             d_codes = keep.tile([P, S], U32, name=name + "_d_codes", align_bytes=64)
-            nc.vector.tensor_copy(
-                d_codes[:].rearrange("p (t c i) -> p c t i", t=PACK, i=4),
-                d_picked[:].rearrange("p (c i t) -> p c t i", t=PACK, i=4),
-            )
+
+            def tokens():
+                nc.vector.tensor_copy(x_codes[:], x_word_table[:].indirect(x_list[:]))
+                nc.vector.tensor_copy(x_plane[:], x_byte_table[:].indirect(x_list[:]))
+
+            def codewords():
+                nc.vector.tensor_copy(d_picked[:], d_word_table[:].indirect(d_list[:]))
+                nc.vector.tensor_copy(
+                    d_codes[:].rearrange("p (t c i) -> p c t i", t=PACK, i=4),
+                    d_picked[:].rearrange("p (c i t) -> p c t i", t=PACK, i=4),
+                )
+
+            for step in (tokens, codewords) if tokens_first else (codewords, tokens):
+                step()
             banks = []
             for t in range(PACK):
                 bank = mm.tile([P, S], F32, name="bank")
@@ -128,7 +135,7 @@ def tile_picked_pqjshareghardkmax_none_po_kernel(
             plane = keep.tile([P, S], U8, name=name + "_plane", align_bytes=64)
             return grouped, codes, plane
 
-        a_banks = first_product(k1_list, offs_list, "a", {"d_picked": 2048, "d_bytes": 5184, "x_plane": 5696, "x_codes": 6208})
+        a_banks = first_product(k1_list, offs_list, "a", {"d_picked": 2048, "d_bytes": 8256, "x_plane": 5696, "x_codes": 6208}, True)
         n2_list = load_list(n2, "n2_list")
         ex = []
         ex_window = []
@@ -139,30 +146,37 @@ def tile_picked_pqjshareghardkmax_none_po_kernel(
             ex_window.append(window)
             ex.append(window[:, 0:S])
 
-        b_banks = first_product(k2_list, two_list, "b", {"d_picked": 64, "d_bytes": 2112, "x_plane": 2624, "x_codes": 3136})
+        b_banks = first_product(k2_list, two_list, "b", {"d_picked": 64, "d_bytes": 2112, "x_plane": 2624, "x_codes": 3136}, False)
         n3_list = load_list(n3, "n3_list")
         n4_list = load_list(n4, "n4_list")
         n5_list = load_list(n5, "n5_list")
-        gains = picked.tile([P, 2, 8], F32, name="gains", align_bytes=64, offset=5184)
+        gains = picked.tile([P, 2, 8], F32, name="gains", align_bytes=64, offset=5696)
         gn_rows = gains[:, 0, 0:PACK]
         nc.sync.dma_start(gn_rows[:], gn.rearrange("(p t) o -> p (t o)", t=PACK))
         gm_rows = gains[:, 1, 0:PACK]
         nc.sync.dma_start(gm_rows[:], gm.rearrange("(p t) o -> p (t o)", t=PACK))
-        w_bytes = picked.tile([P, 2, S], U8, name="w_bytes", align_bytes=64, offset=5696)
+        w_bytes = picked.tile([P, 2, S], U8, name="w_bytes", align_bytes=64, offset=8256)
         w_raw = picked.tile([P, 2, 2 * S], U8, name="w_raw", align_bytes=64, offset=0)
         for w, words in enumerate((w1_words, w2_words)):
             nc.sync.dma_start(w_raw[:, w, :].bitcast(I32), words[0].bitcast(I32))
         for w, scales in enumerate((w1_scales, w2_scales)):
             load_plane(w_bytes[:, w, :], scales, S)
+        w_planes = keep.tile([P, 2, S], U8, name="w_planes", align_bytes=64)
+        for w in range(2):
+            for t in range(PACK):
+                nc.gpsimd.tensor_copy(
+                    w_planes[:, w, t * P : (t + 1) * P], w_bytes[:, w, :].rearrange("p (m t) -> p t m", t=PACK)[:, t, :]
+                )
 
         looked = [keep.tile([P, 2, S], F32, name="ex_looked%d" % t) for t in range(PACK)]
         b_window = [keep.tile([P, B_WIDTH], F32, name="b%d" % t) for t in range(PACK)]
         for window in b_window:
             nc.gpsimd.memset(window[:, S:], 0.0)
         b = [window[:, 0:S] for window in b_window]
-        mb = [keep.tile([P, S, 2], F32, name="mb%d" % t, align_bytes=64) for t in range(PACK)]
+        members_of = keep.tile([P, PACK, S, 2], F32, name="members_of")
+        low = keep.tile([P, PACK, S], F32, name="low")
         high = keep.tile([P, PACK, S], F32, name="high", align_bytes=64)
-        gap = keep.tile([P, PACK, S], F32, name="gap")
+        gap = picked.tile([P, PACK, S], F32, name="gap", align_bytes=64, offset=8256)
         gate = keep.tile([P, PACK, S], F32, name="gate")
         z_planes = keep.tile([P, PACK, S], BF16, name="z_planes")
         z2_planes = keep.tile([P, PACK, S], BF16, name="z2_planes")
@@ -172,15 +186,16 @@ def tile_picked_pqjshareghardkmax_none_po_kernel(
                 gather(engine, looked[t][:, n, :], ex_window[t], lst[:])
 
         def look_up_b(engine, t):
-            flat = mb[t][:].rearrange("p j e -> p (j e)")
+            flat = members_of[:, t, :, :].rearrange("p j e -> p (j e)")
             for start in (0, S):
                 gather(engine, flat[:, start : start + S], b_window[t], cols(n3_list, start, S))
 
-        def members(t):
-            nc.vector.tensor_tensor(high[:, t, :], mb[t][:, :, 0], mb[t][:, :, 1], ALU.max)
-            low = ring.tile([P, S], F32, name="low")
-            nc.vector.tensor_tensor(low[:], mb[t][:, :, 0], mb[t][:, :, 1], ALU.min)
-            nc.vector.tensor_tensor(gap[:, t, :], b[t][:], low[:], ALU.subtract)
+        def members(lo, hi):
+            first, second = members_of[:, lo:hi, :, 0], members_of[:, lo:hi, :, 1]
+            nc.vector.tensor_tensor(high[:, lo:hi, :], first, second, ALU.max)
+            nc.vector.tensor_tensor(low[:, lo:hi, :], first, second, ALU.min)
+            for t in range(lo, hi):
+                nc.gpsimd.tensor_tensor(gap[:, t, :], b[t][:], low[:, t, :], ALU.subtract)
 
         def share(t):
             den = mm.tile([P, S], F32, name="bank")
@@ -189,67 +204,53 @@ def tile_picked_pqjshareghardkmax_none_po_kernel(
                 terms = (ex[t][:, blk], looked[t][:, 0, blk], looked[t][:, 1, blk])
                 for n, term in enumerate(terms):
                     nc.tensor.matmul(den[:, blk], term, ident[:], start=(n == 0), stop=(n == 2), is_transpose=True)
-            root = ring.tile([P, PACK, P], F32, name="root", bufs=4)
-            nc.scalar.activation(root[:], den[:].rearrange("p (c j) -> p c j", j=P), ACT.Abs_reciprocal_sqrt, scale=0.5)
+            root = gate[:].rearrange("p t (h j) -> p (t h) j", h=2)[:, :, t * 64 : (t + 1) * 64]
+            nc.scalar.activation(root, den[:].rearrange("p (c j) -> p c j", j=64), ACT.Abs_reciprocal_sqrt, scale=0.5)
+            inv = ring.tile([P, S], F32, name="inv", bufs=4)
+            nc.scalar.activation(inv[:].rearrange("p (c j) -> p c j", j=64), root, ACT.Square)
             back = turn.tile([P, S], F32, name="back", bufs=4)
             for c in range(PACK):
-                nc.tensor.transpose(back[:, c * P : (c + 1) * P], root[:, c, :], ident[:])
-            return back
+                blk = slice(c * P, (c + 1) * P)
+                nc.tensor.transpose(back[:, blk], inv[:, blk], ident[:])
+            nc.vector.scalar_tensor_tensor(z_planes[:, t, :], back[:], gn_rows[:, t : t + 1], ex[t][:], ALU.mult, ALU.mult)
 
-        def weigh(t, back):
-            inv = gate[:].rearrange("p t (h j) -> p (t h) j", h=2)[:, :, t * 64 : (t + 1) * 64]
-            nc.scalar.activation(inv, back[:].rearrange("p (c j) -> p c j", j=64), ACT.Square)
-            nc.vector.scalar_tensor_tensor(z_planes[:, t, :].rearrange("p (c j) -> p c j", j=64), inv, gn_rows[:, t : t + 1], ex[t][:].rearrange("p (c j) -> p c j", j=64), ALU.mult, ALU.mult)
+        def scale_b(t):
+            nc.scalar.activation(b[t][:], b_banks[t][:], ACT.Copy, scale=0.0625)
 
         look_up_ex("vector", 0)
         look_up_ex("scalar", 1)
+        nc.vector.tensor_scalar(b[0][:], b_banks[0][:], 0.0625, None, ALU.mult)
         look_up_ex("scalar", 2)
-        for t in range(2):
-            nc.vector.tensor_scalar(b[t][:], b_banks[t][:], 0.0625, None, ALU.mult)
+        scale_b(1)
+        scale_b(2)
+        scale_b(3)
         look_up_ex("scalar", 3)
-        for t in range(2, PACK):
-            nc.scalar.activation(b[t][:], b_banks[t][:], ACT.Copy, scale=0.0625)
-        look_up_b("vector", 0)
-        members(0)
-        look_up_b("scalar", 2)
-        look_up_b("vector", 1)
-        members(1)
-        members(2)
-        w_planes = keep.tile([P, 2, S], U8, name="w_planes", tag="mb2", align_bytes=64)
-        for w in range(2):
-            nc.vector.tensor_copy(
-                w_planes[:, w, :].rearrange("p (t c i) -> p c t i", t=PACK, i=16),
-                w_bytes[:, w, :].rearrange("p (c i t) -> p c t i", t=PACK, i=16),
-            )
-        backs = [share(t) for t in range(PACK)]
-        for t in range(PACK):
-            weigh(t, backs[t])
+        for t in range(2):
+            look_up_b("vector", t)
+            members(t, t + 1)
         look_up_b("scalar", 3)
-        w_codes = []
-
-        def deal_weights(w, tag):
-            dealt = keep.tile([P, 2 * S], U8, name="w_codes%d" % w, tag=tag, align_bytes=64)
-            nc.scalar.copy(
-                dealt[:].bitcast(U16).rearrange("p (t c i) -> p c t i", t=PACK, i=8),
-                w_raw[:, w, :].bitcast(U16).rearrange("p (c i t) -> p c t i", t=PACK, i=8),
-            )
-            w_codes.append(dealt)
-
-        deal_weights(0, "w_codes0")
+        look_up_b("vector", 2)
+        members(2, PACK)
+        for t in range(PACK):
+            share(t)
         z_grouped, z_codes, z_plane = mx_tiles("z")
         interleave("vector", z_grouped, z_planes, 0, S)
         quantize(z_codes, z_plane, z_grouped, 0, S)
-        members(3)
 
         for half in range(2):
             lo, hi = half * HALF, (half + 1) * HALF
             for t in range(PACK):
                 nc.scalar.activation(gate[:, t, lo:hi], high[:, t, lo:hi], ACT.Sigmoid)
-        deal_weights(1, "high")
+        w_codes = keep.tile([P, 2, 2 * S], U8, name="w_codes", tag="high", align_bytes=64)
+        for w in range(2):
+            nc.scalar.copy(
+                w_codes[:, w, :].bitcast(U16).rearrange("p (t c i) -> p c t i", t=PACK, i=8),
+                w_raw[:, w, :].bitcast(U16).rearrange("p (c i t) -> p c t i", t=PACK, i=8),
+            )
 
         def second_product(bank, t, w, codes, plane, lo):
             nc.tensor.matmul_mx(
-                bank[:], lhsT=w_codes[w][:, 2 * t * P : 2 * (t + 1) * P].bitcast(FP4X4),
+                bank[:], lhsT=w_codes[:, w, 2 * t * P : 2 * (t + 1) * P].bitcast(FP4X4),
                 lhsT_scale=w_planes[:, w, t * P : (t + 1) * P],
                 rhs=codes[:, lo : lo + HALF].bitcast(FP8X4), rhs_scale=plane[:, lo : lo + HALF],
                 start=(w == 0), stop=(w == 1),
@@ -271,7 +272,7 @@ def tile_picked_pqjshareghardkmax_none_po_kernel(
                 nc.vector.scalar_tensor_tensor(
                     z2_planes[:, t, lo:hi], gap[:, t, lo:hi], gm_rows[:, t : t + 1], gate[:, t, lo:hi], ALU.mult, ALU.mult
                 )
-            interleave("vector", z2_grouped, z2_planes, lo, hi)
+            interleave("vector" if half else "scalar", z2_grouped, z2_planes, lo, hi)
             quantize(z2_codes, z2_plane, z2_grouped, lo, hi)
             for t in range(PACK):
                 second_product(h_banks[half][t], t, 1, z2_codes, z2_plane, lo)
@@ -281,45 +282,40 @@ def tile_picked_pqjshareghardkmax_none_po_kernel(
         out_rows = out_0.rearrange("(p t) j -> p t j", t=PACK)
         y_planes = keep.tile([P, PACK, S], BF16, name="y_planes")
 
-        def fetch(engine, t, pa, old):
-            if engine == "vector":
-                nc.vector.tensor_copy(h[t][:, HALF:S], h_banks[1][t][:])
-            else:
-                nc.scalar.copy(h[t][:, HALF:S], h_banks[1][t][:])
-            gather(engine, pa, h[t], n5_list[:])
-            gather(engine, old, h[t], n4_list[:])
-
-        def larger(ra, pa, old):
-            nc.vector.scalar_tensor_tensor(ra, old, 0.5, pa, ALU.mult, ALU.max)
-
-        old_even = keep.tile([P, 2, U], F32, name="old_even")
-        fetched = [keep.tile([P, 2, U], F32, name="fetched%d" % t) for t in (1, 3)]
-        ra_odd = keep.tile([P, 2, U], F32, name="ra_odd")
-        pa0 = keep.tile([P, U], F32, name="pa0")
-        fetch("vector", 0, pa0[:], old_even[:, 0, :])
-        fetch("scalar", 1, fetched[0][:, 0, :], fetched[0][:, 1, :])
-        larger(ra_odd[:, 0, :], fetched[0][:, 0, :], fetched[0][:, 1, :])
-        pa2 = keep.tile([P, U], F32, name="pa2", tag="fetched1")
-        fetch("vector", 2, pa2[:], old_even[:, 1, :])
-        fetch("scalar", 3, fetched[1][:, 0, :], fetched[1][:, 1, :])
-        larger(ra_odd[:, 1, :], fetched[1][:, 0, :], fetched[1][:, 1, :])
-        ra_even = keep.tile([P, 2, U], F32, name="ra_even", tag="fetched3")
-        larger(ra_even[:, 0, :], pa0[:], old_even[:, 0, :])
-        larger(ra_even[:, 1, :], pa2[:], old_even[:, 1, :])
         for t in range(PACK):
             if t % 2:
-                nc.scalar.activation(h[t][:].indirect(n4_list[:]), ra_odd[:, t // 2, :], ACT.Copy)
+                nc.scalar.copy(h[t][:, HALF:S], h_banks[1][t][:])
             else:
-                nc.vector.tensor_copy(h[t][:].indirect(n4_list[:]), ra_even[:, t // 2, :])
-            nc.sync.dma_start(out_rows[:, t, :], h[t][:])
-        for t in (1, 3, 0):
-            nc.scalar.copy(y_planes[:, t, :], h[t][:])
+                nc.vector.tensor_copy(h[t][:, HALF:S], h_banks[1][t][:])
+        slot = (1, 0, 2, 3)
+        pa = keep.tile([P, PACK, U], F32, name="pa")
+        old = keep.tile([P, PACK, U], F32, name="old")
+        for t in range(PACK):
+            gather("scalar" if t % 2 else "vector", pa[:, slot[t], :], h[t], n5_list[:])
+            gather("scalar" if t else "vector", old[:, slot[t], :], h[t], n4_list[:])
+        ra = keep.tile([P, 3, U], F32, name="ra")
+        for pair in range(2):
+            both = slice(2 * pair, 2 * pair + 2)
+            nc.vector.scalar_tensor_tensor(ra[:, pair : pair + 2, :], old[:, both, :], 0.5, pa[:, both, :], ALU.mult, ALU.max)
+            even, odd = 2 * pair, 2 * pair + 1
+            nc.vector.tensor_copy(h[even][:].indirect(n4_list[:]), ra[:, 1, :])
+            nc.scalar.activation(h[odd][:].indirect(n4_list[:]), ra[:, 2 * pair, :], ACT.Copy)
+            for t in (even, odd):
+                nc.sync.dma_start(out_rows[:, t, :], h[t][:])
+        for t in range(2):
+            nc.gpsimd.tensor_scalar(y_planes[:, t, :], h[t][:], 1.0, 0.0, ALU.mult, ALU.add)
         nc.vector.tensor_copy(y_planes[:, 2, :], h[2][:])
+        for lo in (0, HALF):
+            nc.scalar.copy(y_planes[:, 3, lo : lo + HALF], h[3][:, lo : lo + HALF])
         y_grouped, y_codes, y_plane = mx_tiles("y")
-        interleave("vector", y_grouped, y_planes, 0, S - SCALAR_SHARE)
-        interleave("scalar", y_grouped, y_planes, S - SCALAR_SHARE, S)
-        quantize(y_codes, y_plane, y_grouped, 0, S)
-        nc.sync.dma_start(out_1[0].rearrange("p n t -> p (n t)").bitcast(I32), y_codes[:].bitcast(I32))
+        out_words = out_1[0].rearrange("p n t -> p (n t)").bitcast(I32)
+        interleave("vector", y_grouped, y_planes, 0, HALF)
+        interleave("scalar", y_grouped, y_planes, HALF, HALF + SCALAR_SHARE)
+        quantize(y_codes, y_plane, y_grouped, 0, HALF)
+        nc.sync.dma_start(out_words[:, 0:HALF], y_codes[:, 0:HALF].bitcast(I32))
+        interleave("vector", y_grouped, y_planes, HALF + SCALAR_SHARE, S)
+        quantize(y_codes, y_plane, y_grouped, HALF, S)
+        nc.sync.dma_start(out_words[:, HALF:S], y_codes[:, HALF:S].bitcast(I32))
         for q in range(4):
             queue = nc.scalar if q % 2 else nc.sync
             queue.dma_start(out_2[0, 4 * q : 4 * q + 4, :].bitcast(I32), y_plane[32 * q : 32 * q + 4, :].bitcast(I32))

@@ -20,10 +20,30 @@ S = 512
 T = 1024
 G = 2048
 U = 384
-HALF = 256
-B_WIDTH = 544
+HALF = S // 2
+EX_WIDTH = 2 * S
+B_WIDTH = S + 32
 SCALAR_SHARE = 160
-FLOPS = 4 * 2 * 512 * 512 * 512
+LINE = 16
+FLOPS = 4 * 2 * S * S * S
+
+WORDS = 4 * S
+BYTES = S
+TOUCH = 64
+EX_GAINED_AT = 0
+W_PLANES_AT = EX_GAINED_AT + PACK * WORDS
+B_PICKED_AT = W_PLANES_AT - TOUCH
+B_BYTES_AT = B_PICKED_AT + WORDS
+A_PICKED_AT = B_BYTES_AT - TOUCH
+B_X_PLANE_AT = B_BYTES_AT + BYTES
+B_X_CODES_AT = B_X_PLANE_AT + BYTES
+A_X_PLANE_AT = B_X_CODES_AT + WORDS
+A_X_CODES_AT = A_X_PLANE_AT + BYTES
+A_BYTES_AT = A_X_CODES_AT + WORDS
+W_WORDS_AT = A_X_CODES_AT
+GAINS_AT = A_BYTES_AT
+W_BYTES_AT = GAINS_AT + TOUCH
+GAP_AT = W_BYTES_AT
 
 
 def tile_picked_pqjshareghardkmax_none_po_kernel(
@@ -33,18 +53,22 @@ def tile_picked_pqjshareghardkmax_none_po_kernel(
     nc = tc.nc
     with ExitStack() as ctx:
         keep = ctx.enter_context(tc.tile_pool(name="keep", bufs=1))
-        picked = ctx.enter_context(tc.tile_pool(name="picked", bufs=1))
-        ring = ctx.enter_context(tc.tile_pool(name="ring", bufs=2))
-        mm = ctx.enter_context(tc.psum_pool(name="mm", bufs=4))
-        turn = ctx.enter_context(tc.psum_pool(name="turn", bufs=2))
+        reused = ctx.enter_context(tc.tile_pool(name="reused", bufs=1))
+        sums = ctx.enter_context(tc.psum_pool(name="sums", bufs=PACK))
+        turned = ctx.enter_context(tc.psum_pool(name="turned", bufs=PACK))
+
+        def reused_tile(shape, dtype, name, offset):
+            return reused.tile(shape, dtype, name=name, align_bytes=64, offset=offset)
 
         def load_list(src, name):
             tile = keep.tile(list(src.shape), U16, name=name)
             nc.sync.dma_start(tile[:], src)
             return tile
 
-        def cols(lst, start, count):
-            return lst[:, start // 16 : (start + count) // 16]
+        def load_words(words, width, name):
+            tile = keep.tile([P, width], U32, name=name)
+            nc.sync.dma_start(tile[:].bitcast(I32), words[0].rearrange("p n t -> p (n t)").bitcast(I32))
+            return tile
 
         def load_plane(dst, scales, width):
             rows = scales[0].bitcast(I32)
@@ -54,54 +78,84 @@ def tile_picked_pqjshareghardkmax_none_po_kernel(
                     rows[4 * q : 4 * q + 4, :].unsqueeze(0).to_broadcast([8, 4, width // 4]),
                 )
 
+        def dealt_views(dst, src, run):
+            return (
+                dst.rearrange("p (t c i) -> p c t i", t=PACK, i=run),
+                src.rearrange("p (c i t) -> p c t i", t=PACK, i=run),
+            )
+
+        def gather(engine, out, window, offsets):
+            if engine == "vector":
+                nc.vector.tensor_copy(out, window[:].indirect(offsets))
+            else:
+                nc.scalar.activation(out, window[:].indirect(offsets), ACT.Copy)
+
+        def woven(ap, pattern):
+            return ap.rearrange(pattern + " -> p c t i", t=PACK, i=4)
+
+        def interleave(engine, grouped, row_tiles, lo, hi):
+            dst = woven(grouped[:, lo:hi, :], "p (c i) t")
+            src = woven(row_tiles[:, :, lo:hi], "p t (c i)")
+            if engine == "vector":
+                nc.vector.tensor_copy(dst, src)
+            else:
+                nc.scalar.copy(dst, src)
+
+        def mx_tiles(name):
+            grouped = keep.tile([P, S, PACK], BF16, name=name + "_grouped", align_bytes=64)
+            codes = keep.tile([P, S], U32, name=name + "_codes", align_bytes=64)
+            plane = keep.tile([P, S], U8, name=name + "_plane", align_bytes=64)
+            return grouped, codes, plane
+
+        def quantize(codes, plane, grouped, lo, hi):
+            nc.vector.quantize_mx(
+                codes[:, lo:hi].bitcast(FP8X4), plane[:, lo:hi], grouped[:, lo:hi, :].rearrange("p j t -> p (j t)")
+            )
+
         k1_list = load_list(k1, "k1_list")
         d_byte_table = keep.tile([P, G], U8, name="d_byte_table")
-        nc.sync.dma_start(d_byte_table[:].bitcast(I32), d_scales[0].bitcast(I32).unsqueeze(1).to_broadcast([16, 8, G // 4]))
+        nc.sync.dma_start(
+            d_byte_table[:].bitcast(I32), d_scales[0].bitcast(I32).unsqueeze(1).to_broadcast([16, 8, G // 4])
+        )
         offs_list = load_list(offs, "offs_list")
         x_byte_table = keep.tile([P, T], U8, name="x_byte_table")
         load_plane(x_byte_table, x_scales, T)
-        x_word_table = keep.tile([P, T], U32, name="x_word_table")
-        nc.sync.dma_start(x_word_table[:].bitcast(I32), x_words[0].rearrange("p n t -> p (n t)").bitcast(I32))
+        x_word_table = load_words(x_words, T, "x_word_table")
         k2_list = load_list(k2, "k2_list")
         two_list = load_list(two, "two_list")
         n1_list = load_list(n1, "n1_list")
-        d_word_table = keep.tile([P, G], U32, name="d_word_table")
-        nc.sync.dma_start(d_word_table[:].bitcast(I32), d_words[0].rearrange("p n t -> p (n t)").bitcast(I32))
+        d_word_table = load_words(d_words, G, "d_word_table")
 
         ident = keep.tile([P, P], F32, name="ident")
         make_identity(nc, ident[:])
 
-        def first_product(d_list, x_list, name, place, tokens_first):
-            d_bytes = picked.tile([P, S], U8, name=name + "_d_bytes", align_bytes=64, offset=place["d_bytes"])
+        def pick_codeword_scales(d_list, name, bytes_at):
+            d_bytes = reused_tile([P, S], U8, name + "_d_bytes", bytes_at)
             nc.vector.tensor_copy(d_bytes[:], d_byte_table[:].indirect(d_list[:]))
             d_plane = keep.tile([P, S], U8, name=name + "_d_plane", align_bytes=64)
-            nc.vector.tensor_copy(
-                d_plane[:].rearrange("p (t c i) -> p c t i", t=PACK, i=16),
-                d_bytes[:].rearrange("p (c i t) -> p c t i", t=PACK, i=16),
-            )
+            nc.vector.tensor_copy(*dealt_views(d_plane[:], d_bytes[:], LINE))
             for r in range(1, 4):
                 nc.sync.dma_start(d_plane[r:P:32, :].bitcast(I32), d_plane[8 * r : P : 32, :].bitcast(I32))
-            x_codes = picked.tile([P, S], U32, name=name + "_x_codes", align_bytes=64, offset=place["x_codes"])
-            x_plane = picked.tile([P, S], U8, name=name + "_x_plane", align_bytes=64, offset=place["x_plane"])
-            d_picked = picked.tile([P, S], U32, name=name + "_d_picked", align_bytes=64, offset=place["d_picked"])
+            return d_plane
+
+        def pick_codewords(d_list, name, picked_at):
+            d_picked = reused_tile([P, S], U32, name + "_d_picked", picked_at)
+            nc.vector.tensor_copy(d_picked[:], d_word_table[:].indirect(d_list[:]))
             d_codes = keep.tile([P, S], U32, name=name + "_d_codes", align_bytes=64)
+            nc.vector.tensor_copy(*dealt_views(d_codes[:], d_picked[:], LINE // 4))
+            return d_codes
 
-            def tokens():
-                nc.vector.tensor_copy(x_codes[:], x_word_table[:].indirect(x_list[:]))
-                nc.vector.tensor_copy(x_plane[:], x_byte_table[:].indirect(x_list[:]))
+        def pick_tokens(x_list, name, codes_at, plane_at):
+            x_codes = reused_tile([P, S], U32, name + "_x_codes", codes_at)
+            nc.vector.tensor_copy(x_codes[:], x_word_table[:].indirect(x_list[:]))
+            x_plane = reused_tile([P, S], U8, name + "_x_plane", plane_at)
+            nc.vector.tensor_copy(x_plane[:], x_byte_table[:].indirect(x_list[:]))
+            return x_codes, x_plane
 
-            def codewords():
-                nc.vector.tensor_copy(d_picked[:], d_word_table[:].indirect(d_list[:]))
-                nc.vector.tensor_copy(
-                    d_codes[:].rearrange("p (t c i) -> p c t i", t=PACK, i=4),
-                    d_picked[:].rearrange("p (c i t) -> p c t i", t=PACK, i=4),
-                )
-
-            for step in (tokens, codewords) if tokens_first else (codewords, tokens):
-                step()
+        def first_product(d_codes, d_plane, x_codes, x_plane):
             banks = []
             for t in range(PACK):
-                bank = mm.tile([P, S], F32, name="bank")
+                bank = sums.tile([P, S], F32, name="sum_bank")
                 m_cols = slice(t * P, (t + 1) * P)
                 nc.tensor.matmul_mx(
                     bank[:], lhsT=d_codes[:, m_cols].bitcast(FP8X4), lhsT_scale=d_plane[:, m_cols],
@@ -110,120 +164,82 @@ def tile_picked_pqjshareghardkmax_none_po_kernel(
                 banks.append(bank)
             return banks
 
-        def gather(engine, out, window, offsets):
-            if engine == "vector":
-                nc.vector.tensor_copy(out, window[:].indirect(offsets))
-            else:
-                nc.scalar.activation(out, window[:].indirect(offsets), ACT.Copy)
-
-        def interleave(engine, grouped, planes, lo, hi):
-            dst = grouped[:, lo:hi, :].rearrange("p (c i) t -> p c t i", i=4)
-            src = planes[:, :, lo:hi].rearrange("p t (c i) -> p c t i", i=4)
-            if engine == "vector":
-                nc.vector.tensor_copy(dst, src)
-            else:
-                nc.scalar.copy(dst, src)
-
-        def quantize(codes, plane, grouped, lo, hi):
-            nc.vector.quantize_mx(
-                codes[:, lo:hi].bitcast(FP8X4), plane[:, lo:hi], grouped[:, lo:hi, :].rearrange("p j t -> p (j t)")
-            )
-
-        def mx_tiles(name):
-            grouped = keep.tile([P, S, PACK], BF16, name=name + "_grouped", align_bytes=64)
-            codes = keep.tile([P, S], U32, name=name + "_codes", align_bytes=64)
-            plane = keep.tile([P, S], U8, name=name + "_plane", align_bytes=64)
-            return grouped, codes, plane
-
-        a_banks = first_product(k1_list, offs_list, "a", {"d_picked": 2048, "d_bytes": 8256, "x_plane": 5696, "x_codes": 6208}, True)
+        a_d_plane = pick_codeword_scales(k1_list, "a", A_BYTES_AT)
+        a_x_codes, a_x_plane = pick_tokens(offs_list, "a", A_X_CODES_AT, A_X_PLANE_AT)
+        a_d_codes = pick_codewords(k1_list, "a", A_PICKED_AT)
+        a_banks = first_product(a_d_codes, a_d_plane, a_x_codes, a_x_plane)
         n2_list = load_list(n2, "n2_list")
-        ex = []
-        ex_window = []
+        ex_window = [keep.tile([P, EX_WIDTH], F32, name="ex%d" % t) for t in range(PACK)]
+        ex = [window[:, 0:S] for window in ex_window]
         for t in range(PACK):
-            window = keep.tile([P, 2 * S], F32, name="ex%d" % t)
-            (nc.gpsimd if t % 2 else nc.vector).memset(window[:, S:], 0.0)
-            nc.scalar.activation(window[:, 0:S], a_banks[t][:], ACT.Exp, scale=0.03125)
-            ex_window.append(window)
-            ex.append(window[:, 0:S])
+            (nc.gpsimd if t % 2 else nc.vector).memset(ex_window[t][:, S:], 0.0)
+            nc.scalar.activation(ex[t], a_banks[t][:], ACT.Exp, scale=0.5 * 0.0625)
 
-        b_banks = first_product(k2_list, two_list, "b", {"d_picked": 64, "d_bytes": 2112, "x_plane": 2624, "x_codes": 3136}, False)
+        b_d_plane = pick_codeword_scales(k2_list, "b", B_BYTES_AT)
+        b_d_codes = pick_codewords(k2_list, "b", B_PICKED_AT)
+        b_x_codes, b_x_plane = pick_tokens(two_list, "b", B_X_CODES_AT, B_X_PLANE_AT)
+        b_banks = first_product(b_d_codes, b_d_plane, b_x_codes, b_x_plane)
         n3_list = load_list(n3, "n3_list")
         n4_list = load_list(n4, "n4_list")
         n5_list = load_list(n5, "n5_list")
-        gains = picked.tile([P, 2, 8], F32, name="gains", align_bytes=64, offset=5696)
-        gn_rows = gains[:, 0, 0:PACK]
-        nc.sync.dma_start(gn_rows[:], gn.rearrange("(p t) o -> p (t o)", t=PACK))
-        gm_rows = gains[:, 1, 0:PACK]
-        nc.sync.dma_start(gm_rows[:], gm.rearrange("(p t) o -> p (t o)", t=PACK))
-        w_bytes = picked.tile([P, 2, S], U8, name="w_bytes", align_bytes=64, offset=8256)
-        w_raw = picked.tile([P, 2, 2 * S], U8, name="w_raw", align_bytes=64, offset=0)
-        for w, words in enumerate((w1_words, w2_words)):
-            nc.sync.dma_start(w_raw[:, w, :].bitcast(I32), words[0].bitcast(I32))
+
+        gains = reused_tile([P, 2, 8], F32, "gains", GAINS_AT)
+        gn_rows, gm_rows = gains[:, 0, 0:PACK], gains[:, 1, 0:PACK]
+        nc.sync.dma_start(gn_rows, gn.rearrange("(p t) o -> p (t o)", t=PACK))
+        nc.sync.dma_start(gm_rows, gm.rearrange("(p t) o -> p (t o)", t=PACK))
+        w_bytes = reused_tile([P, 2, S], U8, "w_bytes", W_BYTES_AT)
+        w_words = reused_tile([P, 2, 2 * S], U8, "w_words", W_WORDS_AT)
         for w, scales in enumerate((w1_scales, w2_scales)):
             load_plane(w_bytes[:, w, :], scales, S)
-        w_planes = keep.tile([P, 2, S], U8, name="w_planes", align_bytes=64)
+        for w, words in enumerate((w1_words, w2_words)):
+            nc.sync.dma_start(w_words[:, w, :].bitcast(I32), words[0].bitcast(I32))
+
+        ex_gained = reused_tile([P, PACK, S], F32, "ex_gained", EX_GAINED_AT)
+        for t in range(PACK):
+            nc.gpsimd.tensor_scalar(ex_gained[:, t, :], ex[t], gn_rows[:, t : t + 1], 0.0, ALU.mult, ALU.add)
+        w_planes = reused_tile([P, 2, S], U8, "w_planes", W_PLANES_AT)
         for w in range(2):
             for t in range(PACK):
                 nc.gpsimd.tensor_copy(
                     w_planes[:, w, t * P : (t + 1) * P], w_bytes[:, w, :].rearrange("p (m t) -> p t m", t=PACK)[:, t, :]
                 )
 
-        looked = [keep.tile([P, 2, S], F32, name="ex_looked%d" % t) for t in range(PACK)]
+        ex_looked = [keep.tile([P, 2, S], F32, name="ex_looked%d" % t) for t in range(PACK)]
         b_window = [keep.tile([P, B_WIDTH], F32, name="b%d" % t) for t in range(PACK)]
+        b = [window[:, 0:S] for window in b_window]
         for window in b_window:
             nc.gpsimd.memset(window[:, S:], 0.0)
-        b = [window[:, 0:S] for window in b_window]
-        members_of = keep.tile([P, PACK, S, 2], F32, name="members_of")
-        low = keep.tile([P, PACK, S], F32, name="low")
-        high = keep.tile([P, PACK, S], F32, name="high", align_bytes=64)
-        gap = picked.tile([P, PACK, S], F32, name="gap", align_bytes=64, offset=8256)
-        gate = keep.tile([P, PACK, S], F32, name="gate")
-        z_planes = keep.tile([P, PACK, S], BF16, name="z_planes")
-        z2_planes = keep.tile([P, PACK, S], BF16, name="z2_planes")
+        mb_place = (0, 1, 1, 2)
+        mb = keep.tile([P, 3, S, 2], F32, name="mb")
+        mx = keep.tile([P, PACK, S], F32, name="mx", align_bytes=64)
+        mn = keep.tile([P, PACK, S], F32, name="mn")
+        gap = reused_tile([P, PACK, S], F32, "gap", GAP_AT)
 
         def look_up_ex(engine, t):
             for n, lst in enumerate((n1_list, n2_list)):
-                gather(engine, looked[t][:, n, :], ex_window[t], lst[:])
-
-        def look_up_b(engine, t):
-            flat = members_of[:, t, :, :].rearrange("p j e -> p (j e)")
-            for start in (0, S):
-                gather(engine, flat[:, start : start + S], b_window[t], cols(n3_list, start, S))
-
-        def members(lo, hi):
-            first, second = members_of[:, lo:hi, :, 0], members_of[:, lo:hi, :, 1]
-            nc.vector.tensor_tensor(high[:, lo:hi, :], first, second, ALU.max)
-            nc.vector.tensor_tensor(low[:, lo:hi, :], first, second, ALU.min)
-            for t in range(lo, hi):
-                nc.gpsimd.tensor_tensor(gap[:, t, :], b[t][:], low[:, t, :], ALU.subtract)
-
-        def share(t):
-            den = mm.tile([P, S], F32, name="bank")
-            for c in range(PACK):
-                blk = slice(c * P, (c + 1) * P)
-                terms = (ex[t][:, blk], looked[t][:, 0, blk], looked[t][:, 1, blk])
-                for n, term in enumerate(terms):
-                    nc.tensor.matmul(den[:, blk], term, ident[:], start=(n == 0), stop=(n == 2), is_transpose=True)
-            root = gate[:].rearrange("p t (h j) -> p (t h) j", h=2)[:, :, t * 64 : (t + 1) * 64]
-            nc.scalar.activation(root, den[:].rearrange("p (c j) -> p c j", j=64), ACT.Abs_reciprocal_sqrt, scale=0.5)
-            inv = ring.tile([P, S], F32, name="inv", bufs=4)
-            nc.scalar.activation(inv[:].rearrange("p (c j) -> p c j", j=64), root, ACT.Square)
-            back = turn.tile([P, S], F32, name="back", bufs=4)
-            for c in range(PACK):
-                blk = slice(c * P, (c + 1) * P)
-                nc.tensor.transpose(back[:, blk], inv[:, blk], ident[:])
-            nc.vector.scalar_tensor_tensor(z_planes[:, t, :], back[:], gn_rows[:, t : t + 1], ex[t][:], ALU.mult, ALU.mult)
+                gather(engine, ex_looked[t][:, n, :], ex_window[t], lst[:])
 
         def scale_b(t):
-            nc.scalar.activation(b[t][:], b_banks[t][:], ACT.Copy, scale=0.0625)
+            nc.scalar.activation(b[t], b_banks[t][:], ACT.Copy, scale=0.0625)
+
+        def look_up_b(engine, t):
+            flat = mb[:, mb_place[t], :, :].rearrange("p j e -> p (j e)")
+            for start in (0, S):
+                gather(engine, flat[:, start : start + S], b_window[t], n3_list[:, start // 16 : (start + S) // 16])
+
+        def members(lo, hi):
+            places = slice(mb_place[lo], mb_place[lo] + hi - lo)
+            nc.vector.tensor_tensor(mx[:, lo:hi, :], mb[:, places, :, 0], mb[:, places, :, 1], ALU.max)
+            nc.vector.tensor_tensor(mn[:, lo:hi, :], mb[:, places, :, 0], mb[:, places, :, 1], ALU.min)
+            for t in range(lo, hi):
+                nc.gpsimd.tensor_tensor(gap[:, t, :], b[t], mn[:, t, :], ALU.subtract)
 
         look_up_ex("vector", 0)
         look_up_ex("scalar", 1)
-        nc.vector.tensor_scalar(b[0][:], b_banks[0][:], 0.0625, None, ALU.mult)
+        nc.vector.tensor_scalar(b[0], b_banks[0][:], 0.0625, None, ALU.mult)
         look_up_ex("scalar", 2)
-        scale_b(1)
-        scale_b(2)
-        scale_b(3)
+        for t in range(1, PACK):
+            scale_b(t)
         look_up_ex("scalar", 3)
         for t in range(2):
             look_up_b("vector", t)
@@ -231,91 +247,117 @@ def tile_picked_pqjshareghardkmax_none_po_kernel(
         look_up_b("scalar", 3)
         look_up_b("vector", 2)
         members(2, PACK)
-        for t in range(PACK):
-            share(t)
+
+        gate = keep.tile([P, PACK, S], F32, name="gate")
+        stripe = S // (2 * PACK)
         z_grouped, z_codes, z_plane = mx_tiles("z")
-        interleave("vector", z_grouped, z_planes, 0, S)
+        for c in range(PACK):
+            block = slice(c * P, (c + 1) * P)
+            den = sums.tile([P, S], F32, name="sum_bank")
+            for t in range(PACK):
+                terms = (ex[t][:, block], ex_looked[t][:, 0, block], ex_looked[t][:, 1, block])
+                for n, term in enumerate(terms):
+                    nc.tensor.matmul(
+                        den[:, t * P : (t + 1) * P], term, ident[:], start=(n == 0), stop=(n == 2), is_transpose=True
+                    )
+            root = gate[:].rearrange("p t (h j) -> p (t h) j", h=2)[:, :, c * stripe : (c + 1) * stripe]
+            nc.scalar.activation(
+                root, den[:].rearrange("p (s j) -> p s j", j=stripe), ACT.Abs_reciprocal_sqrt, scale=0.5
+            )
+            twice_inverse = keep.tile([P, S], F32, name="twice_inverse%d" % c)
+            nc.scalar.activation(twice_inverse[:].rearrange("p (s j) -> p s j", j=stripe), root, ACT.Square)
+            back = turned.tile([P, S], F32, name="turned_bank")
+            for t in range(PACK):
+                nc.tensor.transpose(back[:, t * P : (t + 1) * P], twice_inverse[:, t * P : (t + 1) * P], ident[:])
+            nc.vector.tensor_tensor(
+                woven(z_grouped[:, block, :], "p (c i) t"), woven(back[:], "p (t c i)"),
+                woven(ex_gained[:, :, block], "p t (c i)"), ALU.mult,
+            )
         quantize(z_codes, z_plane, z_grouped, 0, S)
 
-        for half in range(2):
-            lo, hi = half * HALF, (half + 1) * HALF
+        def deal_weight_words(w, tag):
+            codes = keep.tile([P, 2 * S], U8, name="w_codes%d" % w, tag=tag, align_bytes=64)
+            nc.scalar.copy(*dealt_views(codes[:].bitcast(U16), w_words[:, w, :].bitcast(U16), LINE // 2))
+            return codes
+
+        w_codes = [deal_weight_words(0, "w_codes0")]
+
+        halves = (slice(0, HALF), slice(HALF, S))
+        for cols in halves:
             for t in range(PACK):
-                nc.scalar.activation(gate[:, t, lo:hi], high[:, t, lo:hi], ACT.Sigmoid)
-        w_codes = keep.tile([P, 2, 2 * S], U8, name="w_codes", tag="high", align_bytes=64)
-        for w in range(2):
-            nc.scalar.copy(
-                w_codes[:, w, :].bitcast(U16).rearrange("p (t c i) -> p c t i", t=PACK, i=8),
-                w_raw[:, w, :].bitcast(U16).rearrange("p (c i t) -> p c t i", t=PACK, i=8),
-            )
+                nc.scalar.activation(gate[:, t, cols], mx[:, t, cols], ACT.Sigmoid)
+        w_codes.append(deal_weight_words(1, "mx"))
 
-        def second_product(bank, t, w, codes, plane, lo):
-            nc.tensor.matmul_mx(
-                bank[:], lhsT=w_codes[:, w, 2 * t * P : 2 * (t + 1) * P].bitcast(FP4X4),
-                lhsT_scale=w_planes[:, w, t * P : (t + 1) * P],
-                rhs=codes[:, lo : lo + HALF].bitcast(FP8X4), rhs_scale=plane[:, lo : lo + HALF],
-                start=(w == 0), stop=(w == 1),
-            )
+        h_banks = (
+            [turned.tile([P, HALF], F32, name="turned_bank") for t in range(PACK)],
+            [sums.tile([P, HALF], F32, name="sum_bank") for t in range(PACK)],
+        )
 
-        h_banks = [
-            [turn.tile([P, HALF], F32, name="back", bufs=4) for t in range(PACK)],
-            [mm.tile([P, HALF], F32, name="bank") for t in range(PACK)],
-        ]
-        for half in range(2):
+        def second_product(half, w, codes, plane):
             for t in range(PACK):
-                second_product(h_banks[half][t], t, 0, z_codes, z_plane, half * HALF)
+                nc.tensor.matmul_mx(
+                    h_banks[half][t][:], lhsT=w_codes[w][:, 2 * t * P : 2 * (t + 1) * P].bitcast(FP4X4),
+                    lhsT_scale=w_planes[:, w, t * P : (t + 1) * P],
+                    rhs=codes[:, halves[half]].bitcast(FP8X4), rhs_scale=plane[:, halves[half]],
+                    start=(w == 0), stop=(w == 1),
+                )
 
+        for half in range(2):
+            second_product(half, 0, z_codes, z_plane)
+        z2_rows = keep.tile([P, PACK, S], BF16, name="z2_rows")
         z2_grouped, z2_codes, z2_plane = mx_tiles("z2")
-        h = [keep.tile([P, S], F32, name="h%d" % t) for t in range(PACK)]
-        for half in range(2):
-            lo, hi = half * HALF, (half + 1) * HALF
+        for half, cols in enumerate(halves):
             for t in range(PACK):
                 nc.vector.scalar_tensor_tensor(
-                    z2_planes[:, t, lo:hi], gap[:, t, lo:hi], gm_rows[:, t : t + 1], gate[:, t, lo:hi], ALU.mult, ALU.mult
+                    z2_rows[:, t, cols], gap[:, t, cols], gm_rows[:, t : t + 1], gate[:, t, cols], ALU.mult, ALU.mult
                 )
-            interleave("vector" if half else "scalar", z2_grouped, z2_planes, lo, hi)
-            quantize(z2_codes, z2_plane, z2_grouped, lo, hi)
-            for t in range(PACK):
-                second_product(h_banks[half][t], t, 1, z2_codes, z2_plane, lo)
+            interleave("vector" if half else "scalar", z2_grouped, z2_rows, cols.start, cols.stop)
+            quantize(z2_codes, z2_plane, z2_grouped, cols.start, cols.stop)
+            second_product(half, 1, z2_codes, z2_plane)
+        h = [keep.tile([P, S], F32, name="h%d" % t) for t in range(PACK)]
         for t in range(PACK):
-            nc.scalar.copy(h[t][:, 0:HALF], h_banks[0][t][:])
-
-        out_rows = out_0.rearrange("(p t) j -> p t j", t=PACK)
-        y_planes = keep.tile([P, PACK, S], BF16, name="y_planes")
-
+            nc.scalar.copy(h[t][:, halves[0]], h_banks[0][t][:])
         for t in range(PACK):
             if t % 2:
-                nc.scalar.copy(h[t][:, HALF:S], h_banks[1][t][:])
+                nc.scalar.copy(h[t][:, halves[1]], h_banks[1][t][:])
             else:
-                nc.vector.tensor_copy(h[t][:, HALF:S], h_banks[1][t][:])
-        slot = (1, 0, 2, 3)
+                nc.vector.tensor_copy(h[t][:, halves[1]], h_banks[1][t][:])
+
+        fetch_place = (1, 0, 2, 3)
         pa = keep.tile([P, PACK, U], F32, name="pa")
         old = keep.tile([P, PACK, U], F32, name="old")
         for t in range(PACK):
-            gather("scalar" if t % 2 else "vector", pa[:, slot[t], :], h[t], n5_list[:])
-            gather("scalar" if t else "vector", old[:, slot[t], :], h[t], n4_list[:])
+            gather("scalar" if t % 2 else "vector", pa[:, fetch_place[t], :], h[t], n5_list[:])
+            gather("scalar" if t else "vector", old[:, fetch_place[t], :], h[t], n4_list[:])
+        out_rows = out_0.rearrange("(p t) j -> p t j", t=PACK)
         ra = keep.tile([P, 3, U], F32, name="ra")
         for pair in range(2):
-            both = slice(2 * pair, 2 * pair + 2)
-            nc.vector.scalar_tensor_tensor(ra[:, pair : pair + 2, :], old[:, both, :], 0.5, pa[:, both, :], ALU.mult, ALU.max)
             even, odd = 2 * pair, 2 * pair + 1
+            nc.vector.scalar_tensor_tensor(
+                ra[:, pair : pair + 2, :], old[:, even : odd + 1, :], 0.5, pa[:, even : odd + 1, :], ALU.mult, ALU.max
+            )
             nc.vector.tensor_copy(h[even][:].indirect(n4_list[:]), ra[:, 1, :])
             nc.scalar.activation(h[odd][:].indirect(n4_list[:]), ra[:, 2 * pair, :], ACT.Copy)
             for t in (even, odd):
                 nc.sync.dma_start(out_rows[:, t, :], h[t][:])
+
+        y_rows = keep.tile([P, PACK, S], BF16, name="y_rows", tag="pa")
         for t in range(2):
-            nc.gpsimd.tensor_scalar(y_planes[:, t, :], h[t][:], 1.0, 0.0, ALU.mult, ALU.add)
-        nc.vector.tensor_copy(y_planes[:, 2, :], h[2][:])
-        for lo in (0, HALF):
-            nc.scalar.copy(y_planes[:, 3, lo : lo + HALF], h[3][:, lo : lo + HALF])
+            nc.gpsimd.tensor_scalar(y_rows[:, t, :], h[t][:], 1.0, 0.0, ALU.mult, ALU.add)
+        nc.vector.tensor_copy(y_rows[:, 2, :], h[2][:])
+        for cols in halves:
+            nc.scalar.copy(y_rows[:, 3, cols], h[3][:, cols])
         y_grouped, y_codes, y_plane = mx_tiles("y")
         out_words = out_1[0].rearrange("p n t -> p (n t)").bitcast(I32)
-        interleave("vector", y_grouped, y_planes, 0, HALF)
-        interleave("scalar", y_grouped, y_planes, HALF, HALF + SCALAR_SHARE)
+        interleave("vector", y_grouped, y_rows, 0, HALF)
+        interleave("scalar", y_grouped, y_rows, HALF, HALF + SCALAR_SHARE)
         quantize(y_codes, y_plane, y_grouped, 0, HALF)
-        nc.sync.dma_start(out_words[:, 0:HALF], y_codes[:, 0:HALF].bitcast(I32))
-        interleave("vector", y_grouped, y_planes, HALF + SCALAR_SHARE, S)
+        nc.sync.dma_start(out_words[:, halves[0]], y_codes[:, halves[0]].bitcast(I32))
+        interleave("vector", y_grouped, y_rows, HALF + SCALAR_SHARE, S)
         quantize(y_codes, y_plane, y_grouped, HALF, S)
-        nc.sync.dma_start(out_words[:, HALF:S], y_codes[:, HALF:S].bitcast(I32))
+        nc.sync.dma_start(out_words[:, halves[1]], y_codes[:, halves[1]].bitcast(I32))
         for q in range(4):
             queue = nc.scalar if q % 2 else nc.sync
-            queue.dma_start(out_2[0, 4 * q : 4 * q + 4, :].bitcast(I32), y_plane[32 * q : 32 * q + 4, :].bitcast(I32))
+            queue.dma_start(
+                out_2[0, 4 * q : 4 * q + 4, :].bitcast(I32), y_plane[32 * q : 32 * q + 4, :].bitcast(I32)
+            )

from contextlib import ExitStack

import concourse.mybir as mybir
from concourse.masks import make_identity

F32 = mybir.dt.float32
BF16 = mybir.dt.bfloat16
I32 = mybir.dt.int32
U32 = mybir.dt.uint32
U16 = mybir.dt.uint16
U8 = mybir.dt.uint8
FP8X4 = mybir.dt.float8_e4m3fn_x4
FP4X4 = mybir.dt.float4_e2m1fn_x4
ACT = mybir.ActivationFunctionType
ALU = mybir.AluOpType

P = 128
PACK = 4
S = 512
T = 1024
G = 2048
U = 384
HALF = S // 2
EX_WIDTH = 2 * S
B_WIDTH = S + 32
SCALAR_SHARE = 160
LINE = 16
FLOPS = 4 * 2 * S * S * S

WORDS = 4 * S
BYTES = S
TOUCH = 64
EX_GAINED_AT = 0
W_PLANES_AT = EX_GAINED_AT + PACK * WORDS
B_PICKED_AT = W_PLANES_AT - TOUCH
B_BYTES_AT = B_PICKED_AT + WORDS
A_PICKED_AT = B_BYTES_AT - TOUCH
B_X_PLANE_AT = B_BYTES_AT + BYTES
B_X_CODES_AT = B_X_PLANE_AT + BYTES
A_X_PLANE_AT = B_X_CODES_AT + WORDS
A_X_CODES_AT = A_X_PLANE_AT + BYTES
A_BYTES_AT = A_X_CODES_AT + WORDS
W_WORDS_AT = A_X_CODES_AT
GAINS_AT = A_BYTES_AT
W_BYTES_AT = GAINS_AT + TOUCH
GAP_AT = W_BYTES_AT


def tile_picked_pqjshareghardkmax_none_po_kernel(
    tc, x_words, x_scales, d_words, d_scales, gn, gm, w1_words, w1_scales, w2_words, w2_scales,
    offs, k1, two, k2, n1, n2, n3, n4, n5, out_0, out_1, out_2,
):
    nc = tc.nc
    with ExitStack() as ctx:
        keep = ctx.enter_context(tc.tile_pool(name="keep", bufs=1))
        reused = ctx.enter_context(tc.tile_pool(name="reused", bufs=1))
        sums = ctx.enter_context(tc.psum_pool(name="sums", bufs=PACK))
        turned = ctx.enter_context(tc.psum_pool(name="turned", bufs=PACK))

        def reused_tile(shape, dtype, name, offset):
            return reused.tile(shape, dtype, name=name, align_bytes=64, offset=offset)

        def load_list(src, name):
            tile = keep.tile(list(src.shape), U16, name=name)
            nc.sync.dma_start(tile[:], src)
            return tile

        def load_words(words, width, name):
            tile = keep.tile([P, width], U32, name=name)
            nc.sync.dma_start(tile[:].bitcast(I32), words[0].rearrange("p n t -> p (n t)").bitcast(I32))
            return tile

        def load_plane(dst, scales, width):
            rows = scales[0].bitcast(I32)
            for q in range(4):
                nc.sync.dma_start(
                    dst[32 * q : 32 * (q + 1), :].bitcast(I32),
                    rows[4 * q : 4 * q + 4, :].unsqueeze(0).to_broadcast([8, 4, width // 4]),
                )

        def dealt_views(dst, src, run):
            return (
                dst.rearrange("p (t c i) -> p c t i", t=PACK, i=run),
                src.rearrange("p (c i t) -> p c t i", t=PACK, i=run),
            )

        def gather(engine, out, window, offsets):
            if engine == "vector":
                nc.vector.tensor_copy(out, window[:].indirect(offsets))
            else:
                nc.scalar.activation(out, window[:].indirect(offsets), ACT.Copy)

        def woven(ap, pattern):
            return ap.rearrange(pattern + " -> p c t i", t=PACK, i=4)

        def interleave(engine, grouped, row_tiles, lo, hi):
            dst = woven(grouped[:, lo:hi, :], "p (c i) t")
            src = woven(row_tiles[:, :, lo:hi], "p t (c i)")
            if engine == "vector":
                nc.vector.tensor_copy(dst, src)
            else:
                nc.scalar.copy(dst, src)

        def mx_tiles(name):
            grouped = keep.tile([P, S, PACK], BF16, name=name + "_grouped", align_bytes=64)
            codes = keep.tile([P, S], U32, name=name + "_codes", align_bytes=64)
            plane = keep.tile([P, S], U8, name=name + "_plane", align_bytes=64)
            return grouped, codes, plane

        def quantize(codes, plane, grouped, lo, hi):
            nc.vector.quantize_mx(
                codes[:, lo:hi].bitcast(FP8X4), plane[:, lo:hi], grouped[:, lo:hi, :].rearrange("p j t -> p (j t)")
            )

        k1_list = load_list(k1, "k1_list")
        d_byte_table = keep.tile([P, G], U8, name="d_byte_table")
        nc.sync.dma_start(
            d_byte_table[:].bitcast(I32), d_scales[0].bitcast(I32).unsqueeze(1).to_broadcast([16, 8, G // 4])
        )
        offs_list = load_list(offs, "offs_list")
        x_byte_table = keep.tile([P, T], U8, name="x_byte_table")
        load_plane(x_byte_table, x_scales, T)
        x_word_table = load_words(x_words, T, "x_word_table")
        k2_list = load_list(k2, "k2_list")
        two_list = load_list(two, "two_list")
        n1_list = load_list(n1, "n1_list")
        d_word_table = load_words(d_words, G, "d_word_table")

        ident = keep.tile([P, P], F32, name="ident")
        make_identity(nc, ident[:])

        def pick_codeword_scales(d_list, name, bytes_at):
            d_bytes = reused_tile([P, S], U8, name + "_d_bytes", bytes_at)
            nc.vector.tensor_copy(d_bytes[:], d_byte_table[:].indirect(d_list[:]))
            d_plane = keep.tile([P, S], U8, name=name + "_d_plane", align_bytes=64)
            nc.vector.tensor_copy(*dealt_views(d_plane[:], d_bytes[:], LINE))
            for r in range(1, 4):
                nc.sync.dma_start(d_plane[r:P:32, :].bitcast(I32), d_plane[8 * r : P : 32, :].bitcast(I32))
            return d_plane

        def pick_codewords(d_list, name, picked_at):
            d_picked = reused_tile([P, S], U32, name + "_d_picked", picked_at)
            nc.vector.tensor_copy(d_picked[:], d_word_table[:].indirect(d_list[:]))
            d_codes = keep.tile([P, S], U32, name=name + "_d_codes", align_bytes=64)
            nc.vector.tensor_copy(*dealt_views(d_codes[:], d_picked[:], LINE // 4))
            return d_codes

        def pick_tokens(x_list, name, codes_at, plane_at):
            x_codes = reused_tile([P, S], U32, name + "_x_codes", codes_at)
            nc.vector.tensor_copy(x_codes[:], x_word_table[:].indirect(x_list[:]))
            x_plane = reused_tile([P, S], U8, name + "_x_plane", plane_at)
            nc.vector.tensor_copy(x_plane[:], x_byte_table[:].indirect(x_list[:]))
            return x_codes, x_plane

        def first_product(d_codes, d_plane, x_codes, x_plane):
            banks = []
            for t in range(PACK):
                bank = sums.tile([P, S], F32, name="sum_bank")
                m_cols = slice(t * P, (t + 1) * P)
                nc.tensor.matmul_mx(
                    bank[:], lhsT=d_codes[:, m_cols].bitcast(FP8X4), lhsT_scale=d_plane[:, m_cols],
                    rhs=x_codes[:].bitcast(FP8X4), rhs_scale=x_plane[:], start=True, stop=True,
                )
                banks.append(bank)
            return banks

        a_d_plane = pick_codeword_scales(k1_list, "a", A_BYTES_AT)
        a_x_codes, a_x_plane = pick_tokens(offs_list, "a", A_X_CODES_AT, A_X_PLANE_AT)
        a_d_codes = pick_codewords(k1_list, "a", A_PICKED_AT)
        a_banks = first_product(a_d_codes, a_d_plane, a_x_codes, a_x_plane)
        n2_list = load_list(n2, "n2_list")
        ex_window = [keep.tile([P, EX_WIDTH], F32, name="ex%d" % t) for t in range(PACK)]
        ex = [window[:, 0:S] for window in ex_window]
        for t in range(PACK):
            (nc.gpsimd if t % 2 else nc.vector).memset(ex_window[t][:, S:], 0.0)
            nc.scalar.activation(ex[t], a_banks[t][:], ACT.Exp, scale=0.5 * 0.0625)

        b_d_plane = pick_codeword_scales(k2_list, "b", B_BYTES_AT)
        b_d_codes = pick_codewords(k2_list, "b", B_PICKED_AT)
        b_x_codes, b_x_plane = pick_tokens(two_list, "b", B_X_CODES_AT, B_X_PLANE_AT)
        b_banks = first_product(b_d_codes, b_d_plane, b_x_codes, b_x_plane)
        n3_list = load_list(n3, "n3_list")
        n4_list = load_list(n4, "n4_list")
        n5_list = load_list(n5, "n5_list")

        gains = reused_tile([P, 2, 8], F32, "gains", GAINS_AT)
        gn_rows, gm_rows = gains[:, 0, 0:PACK], gains[:, 1, 0:PACK]
        nc.sync.dma_start(gn_rows, gn.rearrange("(p t) o -> p (t o)", t=PACK))
        nc.sync.dma_start(gm_rows, gm.rearrange("(p t) o -> p (t o)", t=PACK))
        w_bytes = reused_tile([P, 2, S], U8, "w_bytes", W_BYTES_AT)
        w_words = reused_tile([P, 2, 2 * S], U8, "w_words", W_WORDS_AT)
        for w, scales in enumerate((w1_scales, w2_scales)):
            load_plane(w_bytes[:, w, :], scales, S)
        for w, words in enumerate((w1_words, w2_words)):
            nc.sync.dma_start(w_words[:, w, :].bitcast(I32), words[0].bitcast(I32))

        ex_gained = reused_tile([P, PACK, S], F32, "ex_gained", EX_GAINED_AT)
        for t in range(PACK):
            nc.gpsimd.tensor_scalar(ex_gained[:, t, :], ex[t], gn_rows[:, t : t + 1], 0.0, ALU.mult, ALU.add)
        w_planes = reused_tile([P, 2, S], U8, "w_planes", W_PLANES_AT)
        for w in range(2):
            for t in range(PACK):
                nc.gpsimd.tensor_copy(
                    w_planes[:, w, t * P : (t + 1) * P], w_bytes[:, w, :].rearrange("p (m t) -> p t m", t=PACK)[:, t, :]
                )

        ex_looked = [keep.tile([P, 2, S], F32, name="ex_looked%d" % t) for t in range(PACK)]
        b_window = [keep.tile([P, B_WIDTH], F32, name="b%d" % t) for t in range(PACK)]
        b = [window[:, 0:S] for window in b_window]
        for window in b_window:
            nc.gpsimd.memset(window[:, S:], 0.0)
        mb_place = (0, 1, 1, 2)
        mb = keep.tile([P, 3, S, 2], F32, name="mb")
        mx = keep.tile([P, PACK, S], F32, name="mx", align_bytes=64)
        mn = keep.tile([P, PACK, S], F32, name="mn")
        gap = reused_tile([P, PACK, S], F32, "gap", GAP_AT)

        def look_up_ex(engine, t):
            for n, lst in enumerate((n1_list, n2_list)):
                gather(engine, ex_looked[t][:, n, :], ex_window[t], lst[:])

        def scale_b(t):
            nc.scalar.activation(b[t], b_banks[t][:], ACT.Copy, scale=0.0625)

        def look_up_b(engine, t):
            flat = mb[:, mb_place[t], :, :].rearrange("p j e -> p (j e)")
            for start in (0, S):
                gather(engine, flat[:, start : start + S], b_window[t], n3_list[:, start // 16 : (start + S) // 16])

        def members(lo, hi):
            places = slice(mb_place[lo], mb_place[lo] + hi - lo)
            nc.vector.tensor_tensor(mx[:, lo:hi, :], mb[:, places, :, 0], mb[:, places, :, 1], ALU.max)
            nc.vector.tensor_tensor(mn[:, lo:hi, :], mb[:, places, :, 0], mb[:, places, :, 1], ALU.min)
            for t in range(lo, hi):
                nc.gpsimd.tensor_tensor(gap[:, t, :], b[t], mn[:, t, :], ALU.subtract)

        look_up_ex("vector", 0)
        look_up_ex("scalar", 1)
        nc.vector.tensor_scalar(b[0], b_banks[0][:], 0.0625, None, ALU.mult)
        look_up_ex("scalar", 2)
        for t in range(1, PACK):
            scale_b(t)
        look_up_ex("scalar", 3)
        for t in range(2):
            look_up_b("vector", t)
            members(t, t + 1)
        look_up_b("scalar", 3)
        look_up_b("vector", 2)
        members(2, PACK)

        gate = keep.tile([P, PACK, S], F32, name="gate")
        stripe = S // (2 * PACK)
        z_grouped, z_codes, z_plane = mx_tiles("z")
        for c in range(PACK):
            block = slice(c * P, (c + 1) * P)
            den = sums.tile([P, S], F32, name="sum_bank")
            for t in range(PACK):
                terms = (ex[t][:, block], ex_looked[t][:, 0, block], ex_looked[t][:, 1, block])
                for n, term in enumerate(terms):
                    nc.tensor.matmul(
                        den[:, t * P : (t + 1) * P], term, ident[:], start=(n == 0), stop=(n == 2), is_transpose=True
                    )
            root = gate[:].rearrange("p t (h j) -> p (t h) j", h=2)[:, :, c * stripe : (c + 1) * stripe]
            nc.scalar.activation(
                root, den[:].rearrange("p (s j) -> p s j", j=stripe), ACT.Abs_reciprocal_sqrt, scale=0.5
            )
            twice_inverse = keep.tile([P, S], F32, name="twice_inverse%d" % c)
            nc.scalar.activation(twice_inverse[:].rearrange("p (s j) -> p s j", j=stripe), root, ACT.Square)
            back = turned.tile([P, S], F32, name="turned_bank")
            for t in range(PACK):
                nc.tensor.transpose(back[:, t * P : (t + 1) * P], twice_inverse[:, t * P : (t + 1) * P], ident[:])
            nc.vector.tensor_tensor(
                woven(z_grouped[:, block, :], "p (c i) t"), woven(back[:], "p (t c i)"),
                woven(ex_gained[:, :, block], "p t (c i)"), ALU.mult,
            )
        quantize(z_codes, z_plane, z_grouped, 0, S)

        def deal_weight_words(w, tag):
            codes = keep.tile([P, 2 * S], U8, name="w_codes%d" % w, tag=tag, align_bytes=64)
            nc.scalar.copy(*dealt_views(codes[:].bitcast(U16), w_words[:, w, :].bitcast(U16), LINE // 2))
            return codes

        w_codes = [deal_weight_words(0, "w_codes0")]

        halves = (slice(0, HALF), slice(HALF, S))
        for cols in halves:
            for t in range(PACK):
                nc.scalar.activation(gate[:, t, cols], mx[:, t, cols], ACT.Sigmoid)
        w_codes.append(deal_weight_words(1, "mx"))

        h_banks = (
            [turned.tile([P, HALF], F32, name="turned_bank") for t in range(PACK)],
            [sums.tile([P, HALF], F32, name="sum_bank") for t in range(PACK)],
        )

        def second_product(half, w, codes, plane):
            for t in range(PACK):
                nc.tensor.matmul_mx(
                    h_banks[half][t][:], lhsT=w_codes[w][:, 2 * t * P : 2 * (t + 1) * P].bitcast(FP4X4),
                    lhsT_scale=w_planes[:, w, t * P : (t + 1) * P],
                    rhs=codes[:, halves[half]].bitcast(FP8X4), rhs_scale=plane[:, halves[half]],
                    start=(w == 0), stop=(w == 1),
                )

        for half in range(2):
            second_product(half, 0, z_codes, z_plane)
        z2_rows = keep.tile([P, PACK, S], BF16, name="z2_rows")
        z2_grouped, z2_codes, z2_plane = mx_tiles("z2")
        for half, cols in enumerate(halves):
            for t in range(PACK):
                nc.vector.scalar_tensor_tensor(
                    z2_rows[:, t, cols], gap[:, t, cols], gm_rows[:, t : t + 1], gate[:, t, cols], ALU.mult, ALU.mult
                )
            interleave("vector" if half else "scalar", z2_grouped, z2_rows, cols.start, cols.stop)
            quantize(z2_codes, z2_plane, z2_grouped, cols.start, cols.stop)
            second_product(half, 1, z2_codes, z2_plane)
        h = [keep.tile([P, S], F32, name="h%d" % t) for t in range(PACK)]
        for t in range(PACK):
            nc.scalar.copy(h[t][:, halves[0]], h_banks[0][t][:])
        for t in range(PACK):
            if t % 2:
                nc.scalar.copy(h[t][:, halves[1]], h_banks[1][t][:])
            else:
                nc.vector.tensor_copy(h[t][:, halves[1]], h_banks[1][t][:])

        fetch_place = (1, 0, 2, 3)
        pa = keep.tile([P, PACK, U], F32, name="pa")
        old = keep.tile([P, PACK, U], F32, name="old")
        for t in range(PACK):
            gather("scalar" if t % 2 else "vector", pa[:, fetch_place[t], :], h[t], n5_list[:])
            gather("scalar" if t else "vector", old[:, fetch_place[t], :], h[t], n4_list[:])
        out_rows = out_0.rearrange("(p t) j -> p t j", t=PACK)
        ra = keep.tile([P, 3, U], F32, name="ra")
        for pair in range(2):
            even, odd = 2 * pair, 2 * pair + 1
            nc.vector.scalar_tensor_tensor(
                ra[:, pair : pair + 2, :], old[:, even : odd + 1, :], 0.5, pa[:, even : odd + 1, :], ALU.mult, ALU.max
            )
            nc.vector.tensor_copy(h[even][:].indirect(n4_list[:]), ra[:, 1, :])
            nc.scalar.activation(h[odd][:].indirect(n4_list[:]), ra[:, 2 * pair, :], ACT.Copy)
            for t in (even, odd):
                nc.sync.dma_start(out_rows[:, t, :], h[t][:])

        y_rows = keep.tile([P, PACK, S], BF16, name="y_rows", tag="pa")
        for t in range(2):
            nc.gpsimd.tensor_scalar(y_rows[:, t, :], h[t][:], 1.0, 0.0, ALU.mult, ALU.add)
        nc.vector.tensor_copy(y_rows[:, 2, :], h[2][:])
        for cols in halves:
            nc.scalar.copy(y_rows[:, 3, cols], h[3][:, cols])
        y_grouped, y_codes, y_plane = mx_tiles("y")
        out_words = out_1[0].rearrange("p n t -> p (n t)").bitcast(I32)
        interleave("vector", y_grouped, y_rows, 0, HALF)
        interleave("scalar", y_grouped, y_rows, HALF, HALF + SCALAR_SHARE)
        quantize(y_codes, y_plane, y_grouped, 0, HALF)
        nc.sync.dma_start(out_words[:, halves[0]], y_codes[:, halves[0]].bitcast(I32))
        interleave("vector", y_grouped, y_rows, HALF + SCALAR_SHARE, S)
        quantize(y_codes, y_plane, y_grouped, HALF, S)
        nc.sync.dma_start(out_words[:, halves[1]], y_codes[:, halves[1]].bitcast(I32))
        for q in range(4):
            queue = nc.scalar if q % 2 else nc.sync
            queue.dma_start(
                out_2[0, 4 * q : 4 * q + 4, :].bitcast(I32), y_plane[32 * q : 32 * q + 4, :].bitcast(I32)
            )
